import numpy as np
import ml_dtypes


def mxq(x, axis, fmt="e4m3"):
    dtype, down = {"e4m3": (ml_dtypes.float8_e4m3fn, 7), "e5m2": (ml_dtypes.float8_e5m2, 14)}[fmt]
    v = np.moveaxis(np.asarray(x, np.float32).astype(ml_dtypes.bfloat16).astype(np.float64), axis, -1)
    blocks = v.reshape(v.shape[:-1] + (-1, 32))
    amax = np.abs(blocks).max(-1, keepdims=True)
    byte = np.maximum(np.where(amax > 0, np.frexp(amax)[1] - 1 + 127, 0) - down, 1)
    scale = np.exp2(byte - 127.0)
    codes = (blocks / scale).astype(np.float32).astype(dtype).astype(np.float64)
    return np.moveaxis((codes * scale).reshape(v.shape), -1, axis)


WIDE = False


def mx_kscale(k):
    if not WIDE:
        return np.ones(k)
    levels = np.array([10, -10, 5, -5, 0])
    if k % 512:
        return np.exp2(np.random.permutation(np.resize(levels, k // 32))).repeat(32)
    a = np.empty((k // 512, 16))
    for p in range(k // 512):
        a[p, :8] = np.random.permutation(np.resize(levels, 8))
        for g in range(8):
            far = levels[np.abs(levels - a[p, g]) >= 10]
            a[p, g + 8] = far[np.random.randint(len(far))]
    return np.exp2(a.ravel()).repeat(32)


BF16 = ml_dtypes.bfloat16


def bf(x):
    return np.asarray(x, np.float32).astype(BF16)


def f64(x):
    return np.asarray(x).astype(np.float64)


E2M1 = np.array([0.0, 0.5, 1.0, 1.5, 2.0, 3.0, 4.0, 6.0, -0.0, -0.5, -1.0, -1.5, -2.0, -3.0, -4.0, -6.0])


def pack_weight(w, fmt):
    k, n = w.shape
    w = f64(bf(w)).reshape(k // 32, 32, n)
    amax = np.abs(w).max(1)
    if fmt == "e4m3":
        byte = np.frexp(amax)[1] - 1 + 127 - 7
    else:
        mant, ex = np.frexp(amax / 6.0)
        byte = np.where(mant > 0.5, ex, ex - 1) + 127
    byte = np.clip(np.where(amax > 0, byte, 1), 1, 254)
    scaled = (w * np.exp2(127.0 - byte)[:, None, :]).reshape(k, n).astype(np.float32)
    by_word = np.ascontiguousarray(scaled.reshape(k // 512, 128, 4, n).transpose(0, 1, 3, 2))
    if fmt == "e4m3":
        words = by_word.astype(ml_dtypes.float8_e4m3fn).view(np.uint8)
    else:
        c = by_word.astype(ml_dtypes.float4_e2m1fn).view(np.uint8) & 0xF
        words = c[..., 0::2] | (c[..., 1::2] << 4)
    return np.ascontiguousarray(words), np.ascontiguousarray(byte.astype(np.uint8).reshape(k // 512, 16, n))


def unpack_weight(words, scales, fmt):
    g, p, n, _ = words.shape
    if fmt == "e4m3":
        vals = np.ascontiguousarray(words).view(ml_dtypes.float8_e4m3fn).astype(np.float64)
    else:
        nib = np.empty((g, p, n, 4), np.uint8)
        nib[..., 0::2] = words & 0xF
        nib[..., 1::2] = words >> 4
        vals = E2M1[nib]
    vals = vals * np.repeat(np.exp2(scales.astype(np.float64) - 127.0), 8, axis=1)[..., None]
    return vals.transpose(0, 1, 3, 2).reshape(g * 512, n)
def pack4(w):
    words, scales = pack_weight(w, "e2m1")
    return words.reshape(words.shape[0], 128, -1), scales


def unpack4(words, scales):
    return unpack_weight(words.reshape(words.shape[0], 128, -1, 2), scales, "e2m1")


def planes(Y):
    n, m = Y.shape
    b = f64(bf(Y)).reshape(n // 32, 32, m)
    amax = np.abs(b).max(1)
    byte = np.clip(np.where(amax > 0, np.frexp(amax)[1] - 1 + 127 - 7, 1), 1, 254)
    codes = (b * np.exp2(127.0 - byte)[:, None, :]).reshape(n, m).astype(np.float32).astype(ml_dtypes.float8_e4m3fn).view(np.uint8)
    words = codes.reshape(n // 512, 128, 4, m).transpose(0, 1, 3, 2)
    return np.ascontiguousarray(words), np.ascontiguousarray(byte.astype(np.uint8).reshape(n // 512, 16, m))


S, R, Q, P, N = 512, 512, 1536, 2048, 1536

def setup_inputs():
    rn = np.random.randn
    s_r = mx_kscale(R)
    s_q = mx_kscale(Q)
    t = mx_kscale(P)
    a = bf(rn(S, R) / s_r)
    b = bf(0.8 * rn(R, P) / np.sqrt(R) * s_r[:, None])
    c = bf(rn(S, Q) / s_q)
    d_words, d_scales = pack4(0.8 * rn(Q, P) / np.sqrt(Q) * s_q[:, None])
    ebar = bf(rn(S))
    contrast = bf(np.random.uniform(0.5, 2.0, P) * t)
    gam_words, gam_scales = pack_weight(0.6 * rn(P, N) / np.sqrt(P) / t[:, None], "e4m3")
    v = bf(np.exp(0.8 * rn(N)))
    return dict(a=a, b=b, c=c, d_words=d_words, d_scales=d_scales, ebar=ebar,
                contrast=contrast, gam_words=gam_words, gam_scales=gam_scales, v=v)

def reference(a, b, c, d_words, d_scales, ebar, contrast, gam_words, gam_scales, v):
    d = unpack4(d_words, d_scales)
    gam = unpack_weight(gam_words, gam_scales, "e4m3")
    mean = f64(ebar)[:, None]
    lead = mxq(f64(a), 1, "e4m3") @ mxq(f64(b), 0, "e4m3")
    rest = mxq(f64(c), 1, "e4m3") @ d
    tau = (lead + rest + mean) * f64(contrast)
    y = (mean - (mxq(tau, 1, "e4m3") @ gam)) * f64(v)
    Y = y.T
    words, scales = planes(Y)
    return y, words, scales

@@ -1,0 +1,431 @@
+from contextlib import ExitStack
+
+import concourse.mybir as mybir
+from concourse.masks import make_identity
+
+S, R, Q, PTS, N = 512, 512, 1536, 2048, 1536
+FLOPS = 2 * S * (R + Q) * PTS + 2 * S * PTS * N
+
+F32 = mybir.dt.float32
+BF16 = mybir.dt.bfloat16
+I32 = mybir.dt.int32
+U32 = mybir.dt.uint32
+U8 = mybir.dt.uint8
+FP8X4 = mybir.dt.float8_e4m3fn_x4
+FP4X4 = mybir.dt.float4_e2m1fn_x4
+ALU = mybir.AluOpType
+
+P = 128
+W = 512
+TILES = 4
+BANKS = 8
+C_PASSES = Q // W
+PT_CHUNKS = PTS // W
+N_CHUNKS = N // W
+
+
+def tile_polarisation_green_step_k6_kernel(
+    tc, a, b, c, d_words, d_scales, ebar, contrast, gam_words, gam_scales, v, out_0, out_1, out_2
+):
+    nc = tc.nc
+    with ExitStack() as ctx:
+        keep = ctx.enter_context(tc.tile_pool(name="keep", bufs=1))
+        psum = ctx.enter_context(tc.psum_pool(name="psum", bufs=1))
+        ctx.enter_context(tc.manual_schedule())
+
+        taken = []
+
+        def new_bank():
+            index = len(taken) % BANKS
+            taken.append(index)
+            return psum.tile([P, W], F32, name="bank%d" % index)
+
+        def sb(name, shape, dtype, bufs=1):
+            return keep.tile(shape, dtype, name=name, bufs=bufs, align_bytes=64)
+
+        def copy(engine, out, in_):
+            if engine == "vector":
+                nc.vector.tensor_copy(out=out, in_=in_)
+            else:
+                nc.scalar.copy(out=out, in_=in_)
+
+        def case_rows(ap, m):
+            return ap.rearrange("(h i e) k -> h e i k", h=2, e=2)[m // 2, m % 2]
+
+        ident = sb("ident", [P, P], F32)
+        make_identity(nc, ident[:])
+
+        d_plane0 = sb("d_plane0", [P, C_PASSES, W], U8)
+        d_plane1 = sb("d_plane1", [P, C_PASSES, PTS - W], U8)
+        g_plane = sb("g_plane", [P, N], U8)
+        nc.vector.memset(d_plane0[:].rearrange("p j n -> p (j n)").bitcast(I32), 0)
+        nc.vector.memset(d_plane1[:].rearrange("p j n -> p (j n)").bitcast(I32), 0)
+        nc.vector.memset(g_plane[:].bitcast(I32), 0)
+
+        con_rows = sb("con_rows", [P, PTS // P], BF16)
+        ebar_sb = sb("ebar_sb", [P, TILES], BF16)
+        v_wide = sb("v_wide", [P, N], BF16)
+        v_neg = sb("v_neg", [P, N], BF16)
+        con_wide = sb("con_wide", [P, PTS], BF16)
+        a_sb = [sb("a%d" % m, [P, R], BF16) for m in range(TILES)]
+        c_sb = [sb("c%d" % m, [P, Q], BF16) for m in range(TILES)]
+        b_sb = [sb("b%d" % g, [P, 4, W], BF16) for g in range(PT_CHUNKS)]
+        d_sb = [sb("d%d" % g, [P, C_PASSES, 2 * W], U8) for g in range(PT_CHUNKS)]
+        g_sb = [sb("g%d" % n, [P, PT_CHUNKS, W], U32) for n in range(N_CHUNKS)]
+
+        def load_cases(m):
+            nc.sync.dma_start(out=c_sb[m][:], in_=case_rows(c, m))
+            nc.sync.dma_start(out=a_sb[m][:], in_=case_rows(a, m))
+
+        def load_b(g):
+            nc.sync.dma_start(out=b_sb[g][:], in_=b[:, W * g : W * (g + 1)].rearrange("(p t) n -> p t n", t=4))
+
+        def load_d(g):
+            src = d_words.rearrange("j p n -> p j n")[:, :, 2 * W * g : 2 * W * (g + 1)]
+            nc.sync.dma_start(out=d_sb[g][:].bitcast(I32), in_=src.bitcast(I32))
+
+        def load_d_scales(queue, plane, first, last):
+            for q in range(4):
+                src = d_scales[:, 4 * q : 4 * q + 4, first:last].rearrange("j r n -> r j n")
+                queue.dma_start(out=plane[32 * q : 32 * q + 4, :, :].bitcast(I32), in_=src.bitcast(I32))
+
+        def load_gam(n):
+            src = gam_words.rearrange("g p n t -> p g (n t)")[:, :, 4 * W * n : 4 * W * (n + 1)]
+            nc.sync.dma_start(out=g_sb[n][:].bitcast(I32), in_=src.bitcast(I32))
+
+        nc.sync.dma_start(out=con_rows[:], in_=contrast.rearrange("(p c) -> p c", p=P))
+        load_cases(0)
+        load_b(0)
+        load_d_scales(nc.scalar, d_plane0, 0, W)
+        load_d(0)
+        load_cases(1)
+        nc.sync.dma_start(
+            out=ebar_sb[:].rearrange("i (h e) -> i h e", h=2), in_=ebar.rearrange("(h i e) -> i h e", h=2, e=2)
+        )
+        load_cases(2)
+        load_cases(3)
+        load_b(1)
+        load_d_scales(nc.sync, d_plane1, W, PTS)
+        load_d(1)
+        for g in range(2, PT_CHUNKS):
+            load_b(g)
+            load_d(g)
+        for q in range(4):
+            nc.sync.dma_start(
+                out=g_plane[32 * q : 32 * q + 16, :].bitcast(I32),
+                in_=gam_scales[:, 4 * q : 4 * q + 4, :].bitcast(I32),
+            )
+        load_gam(0)
+        nc.sync.dma_start(out=v_wide[:], in_=v.partition_broadcast(P))
+        load_gam(1)
+        load_gam(2)
+
+        def spread_contrast():
+            words = con_rows[:].bitcast(F32)
+            wide = con_wide[:].bitcast(F32).rearrange("j (g u r) -> j u g r", g=PT_CHUNKS, u=2)
+            for u in range(2):
+                bank = new_bank()
+                for k in range(4):
+                    col = 2 * k + u
+                    nc.tensor.transpose(
+                        bank[:, P * k : P * (k + 1)], words[:, col : col + 1].to_broadcast([P, P]), ident[:]
+                    )
+                nc.scalar.copy(
+                    out=wide[:, u].rearrange("j g (r k) -> j g r k", k=4),
+                    in_=bank[:].rearrange("j (k g r) -> j g r k", k=4, g=PT_CHUNKS),
+                )
+
+        ac_codes = [sb("ac_codes%d" % m, [P, W], U32) for m in range(TILES)]
+        ac_scales = [sb("ac_scales%d" % m, [P, W], U8) for m in range(TILES)]
+        ac_grouped = {}
+
+        def turn_cases(m):
+            grouped = sb("ac_grouped", [P, 4 * W], BF16, bufs=2)
+            ac_grouped[m] = grouped
+            sources = [c_sb[m][:, W * j : W * (j + 1)] for j in range(C_PASSES)] + [a_sb[m][:]]
+            for half in range(2):
+                bank = new_bank()
+                for jj in range(2):
+                    words = sources[2 * half + jj].bitcast(F32)
+                    for u in range(2):
+                        slot = 2 * jj + u
+                        nc.tensor.transpose(bank[:, P * slot : P * (slot + 1)], words[:, u : 2 * P : 2], ident[:])
+                nc.scalar.copy(
+                    out=grouped[:].bitcast(F32)[:, W * half : W * (half + 1)].rearrange("p (j i u) -> p j i u", j=2, u=2),
+                    in_=bank[:].rearrange("p (j u i) -> p j i u", j=2, u=2),
+                )
+
+        def quantise(codes, scales, grouped):
+            nc.vector.quantize_mx(out=codes.bitcast(FP8X4), scales=scales, in_=grouped)
+
+        def quantise_cases(m):
+            quantise(ac_codes[m][:], ac_scales[m][:], ac_grouped[m][:])
+
+        b_codes = [sb("b_codes%d" % g, [P, W], U32) for g in range(PT_CHUNKS)]
+        b_scales = [sb("b_scales%d" % g, [P, W], U8) for g in range(PT_CHUNKS)]
+        b_grouped = {}
+
+        def interleave_b(g, engines):
+            grouped = sb("b_grouped", [P, 4 * W], BF16, bufs=2)
+            b_grouped[g] = grouped
+            share = W // len(engines)
+            for s, engine in enumerate(engines):
+                copy(
+                    engine,
+                    grouped[:, 4 * share * s : 4 * share * (s + 1)].rearrange("p (c i t) -> p c t i", i=4, t=4),
+                    b_sb[g][:, :, share * s : share * (s + 1)].rearrange("p t (c i) -> p c t i", i=4),
+                )
+
+        def quantise_b(g):
+            quantise(b_codes[g][:], b_scales[g][:], b_grouped[g][:])
+
+        strain_bank = {}
+
+        def strain_matmuls(m, g):
+            bank = new_bank()
+            strain_bank[m, g] = bank
+            for j in range(C_PASSES + 1):
+                cols = slice(P * j, P * (j + 1))
+                if j == C_PASSES:
+                    rhs, rhs_scale = b_codes[g][:].bitcast(FP8X4), b_scales[g][:]
+                elif g == 0:
+                    rhs, rhs_scale = d_sb[g][:, j, :].bitcast(FP4X4), d_plane0[:, j, :]
+                else:
+                    rhs, rhs_scale = d_sb[g][:, j, :].bitcast(FP4X4), d_plane1[:, j, W * (g - 1) : W * g]
+                nc.tensor.matmul_mx(
+                    out=bank[:],
+                    lhsT=ac_codes[m][:, cols].bitcast(FP8X4),
+                    lhsT_scale=ac_scales[m][:, cols],
+                    rhs=rhs,
+                    rhs_scale=rhs_scale,
+                    start=(j == 0),
+                    stop=(j == C_PASSES),
+                )
+
+        def sorted_pairs(ap, u):
+            return ap.rearrange("s (p u e) -> s u p e", u=2, e=2)[:, u]
+
+        tau_sb = {}
+
+        def polarise(m, g):
+            tau = sb("tau%d" % m, [P, W], BF16, bufs=2)
+            tau_sb[m, g] = tau
+            for u in range(2):
+                half = slice(W * g + 2 * P * u, W * g + 2 * P * (u + 1))
+                nc.vector.scalar_tensor_tensor(
+                    out=tau[:, 2 * P * u : 2 * P * (u + 1)].rearrange("s (p e) -> s p e", e=2),
+                    in0=sorted_pairs(strain_bank[m, g][:], u),
+                    scalar=ebar_sb[:, m : m + 1],
+                    in1=con_wide[:, half].rearrange("s (p e) -> s p e", e=2),
+                    op0=ALU.add,
+                    op1=ALU.mult,
+                )
+
+        def turn_tile(bank, e, source):
+            words = source[:].bitcast(F32)
+            for u in range(2):
+                slot = 2 * e + u
+                nc.tensor.transpose(bank[:, P * slot : P * (slot + 1)], words[:, P * u : P * (u + 1)], ident[:])
+
+        tau_codes = [sb("tau_codes%d" % g, [P, W], U32) for g in range(PT_CHUNKS)]
+        tau_scales = [sb("tau_scales%d" % g, [P, W], U8) for g in range(PT_CHUNKS)]
+        tau_grouped = {}
+
+        def turn_tau(g, h, engine):
+            bank = new_bank()
+            for e in range(2):
+                turn_tile(bank, e, tau_sb[2 * h + e, g])
+            grouped = sb("tau_grouped%d" % h, [P, 2 * W], BF16, bufs=2)
+            tau_grouped[g, h] = grouped
+            copy(
+                engine,
+                grouped[:].bitcast(F32).rearrange("p (e i u) -> p e i u", e=2, u=2),
+                bank[:].rearrange("p (e u i) -> p e i u", e=2, u=2),
+            )
+
+        def quantise_tau(g, h):
+            cols = slice(2 * P * h, 2 * P * (h + 1))
+            quantise(tau_codes[g][:, cols], tau_scales[g][:, cols], tau_grouped[g, h][:])
+
+        green_bank = {}
+
+        def green_matmuls(m, n, passes):
+            if passes[0] == 0:
+                green_bank[m, n] = new_bank()
+            cols = slice(P * m, P * (m + 1))
+            for g in passes:
+                nc.tensor.matmul_mx(
+                    out=green_bank[m, n][:],
+                    lhsT=tau_codes[g][:, cols].bitcast(FP8X4),
+                    lhsT_scale=tau_scales[g][:, cols],
+                    rhs=g_sb[n][:, g, :].bitcast(FP8X4),
+                    rhs_scale=g_plane[4 * g :, W * n : W * (n + 1)],
+                    start=(g == 0),
+                    stop=(g == PT_CHUNKS - 1),
+                )
+
+        y_sb = {}
+        y_half = {}
+
+        def weigh(m, n):
+            y = sb("y%d" % m, [P, W], F32, bufs=2)
+            y_sb[m, n] = y
+            nc.vector.scalar_tensor_tensor(
+                out=y[:],
+                in0=green_bank[m, n][:],
+                scalar=ebar_sb[:, m : m + 1],
+                in1=v_neg[:, W * n : W * (n + 1)],
+                op0=ALU.subtract,
+                op1=ALU.mult,
+            )
+            nc.sync.dma_start(out=case_rows(out_0, m)[:, W * n : W * (n + 1)], in_=y[:])
+
+        def round_y(m, n):
+            rounded = sb("y_half%d" % m, [P, W], BF16, bufs=2)
+            y_half[m, n] = rounded
+            nc.scalar.copy(
+                out=rounded[:].rearrange("s (u p e) -> s u p e", u=2, e=2),
+                in_=y_sb[m, n][:].rearrange("s (p u e) -> s u p e", u=2, e=2),
+            )
+
+        def weigh_rounded(m, n):
+            rounded = sb("y_half%d" % m, [P, W], BF16, bufs=2)
+            y_half[m, n] = rounded
+            for u in range(2):
+                nc.vector.scalar_tensor_tensor(
+                    out=rounded[:, 2 * P * u : 2 * P * (u + 1)].rearrange("s (p e) -> s p e", e=2),
+                    in0=sorted_pairs(green_bank[m, n][:], u),
+                    scalar=ebar_sb[:, m : m + 1],
+                    in1=sorted_pairs(v_neg[:, W * n : W * (n + 1)], u),
+                    op0=ALU.subtract,
+                    op1=ALU.mult,
+                )
+
+        y_codes = [sb("y_codes%d" % n, [P, W], U32) for n in range(N_CHUNKS)]
+        y_scales = [sb("y_scales%d" % n, [P, W], U8) for n in range(N_CHUNKS)]
+        y_bank = {}
+        y_grouped = {}
+
+        def turn_y(m, n):
+            if m % 2 == 0:
+                y_bank[m // 2, n] = new_bank()
+            turn_tile(y_bank[m // 2, n], m % 2, y_half[m, n])
+
+        def gather_y(h, n):
+            grouped = sb("y_grouped%d" % h, [P, 2 * W], BF16, bufs=2)
+            y_grouped[h, n] = grouped
+            nc.scalar.copy(
+                out=grouped[:].bitcast(F32).rearrange("p (i e u) -> p i e u", e=2, u=2),
+                in_=y_bank[h, n][:].rearrange("p (e u i) -> p i e u", e=2, u=2),
+            )
+
+        def quantise_y(h, n):
+            cols = slice(2 * P * h, 2 * P * (h + 1))
+            quantise(y_codes[n][:, cols], y_scales[n][:, cols], y_grouped[h, n][:])
+            nc.sync.dma_start(
+                out=out_1[n].rearrange("p m t -> p (m t)").bitcast(I32)[:, cols], in_=y_codes[n][:, cols].bitcast(I32)
+            )
+
+        def store_y_scales(n, queues):
+            for q in range(4):
+                queues[q % len(queues)].dma_start(
+                    out=out_2[n, 4 * q : 4 * q + 4, :].bitcast(I32), in_=y_scales[n][32 * q : 32 * q + 4, :].bitcast(I32)
+                )
+
+        spread_contrast()
+        turn_cases(0)
+        interleave_b(0, ["vector"])
+        quantise_cases(0)
+        quantise_b(0)
+        turn_cases(1)
+        quantise_cases(1)
+        strain_matmuls(0, 0)
+        turn_cases(2)
+        polarise(0, 0)
+        quantise_cases(2)
+        strain_matmuls(1, 0)
+        turn_cases(3)
+        polarise(1, 0)
+        quantise_cases(3)
+        interleave_b(1, ["vector", "scalar"])
+        strain_matmuls(2, 0)
+        polarise(2, 0)
+        quantise_b(1)
+        strain_matmuls(3, 0)
+        polarise(3, 0)
+
+        for g in range(1, PT_CHUNKS):
+            more = g + 1 < PT_CHUNKS
+            if more:
+                interleave_b(g + 1, ["scalar"])
+            strain_matmuls(0, g)
+            polarise(0, g)
+            strain_matmuls(1, g)
+            polarise(1, g)
+            turn_tau(g - 1, 0, "scalar")
+            turn_tau(g - 1, 1, "scalar")
+            if more:
+                quantise_b(g + 1)
+            else:
+                nc.vector.tensor_scalar(out=v_neg[:], in0=v_wide[:], scalar1=-1.0, scalar2=None, op0=ALU.mult)
+            strain_matmuls(2, g)
+            quantise_tau(g - 1, 0)
+            polarise(2, g)
+            quantise_tau(g - 1, 1)
+            strain_matmuls(3, g)
+            polarise(3, g)
+
+        last = PT_CHUNKS - 1
+        early = list(range(last))
+        green_matmuls(0, 0, early)
+        green_matmuls(1, 0, early)
+        turn_tau(last, 0, "scalar")
+        turn_tau(last, 1, "vector")
+        quantise_tau(last, 0)
+        quantise_tau(last, 1)
+        green_matmuls(2, 0, early)
+        for m in range(2):
+            green_matmuls(m, 0, [last])
+        for m in range(2):
+            weigh(m, 0)
+            round_y(m, 0)
+        green_matmuls(3, 0, early)
+        for m in range(2, TILES):
+            green_matmuls(m, 0, [last])
+        for m in range(2, TILES):
+            weigh(m, 0)
+            round_y(m, 0)
+
+        every = list(range(PT_CHUNKS))
+        for n in range(1, N_CHUNKS):
+            for m in range(2):
+                green_matmuls(m, n, every)
+                weigh(m, n)
+                round_y(m, n)
+            for m in range(TILES):
+                turn_y(m, n - 1)
+            for h in range(2):
+                gather_y(h, n - 1)
+            green_matmuls(2, n, every)
+            quantise_y(0, n - 1)
+            weigh(2, n)
+            round_y(2, n)
+            quantise_y(1, n - 1)
+            store_y_scales(n - 1, [nc.sync])
+            green_matmuls(3, n, every)
+            if n + 1 < N_CHUNKS:
+                weigh(3, n)
+                round_y(3, n)
+
+        n = N_CHUNKS - 1
+        weigh_rounded(3, n)
+        for m in range(2):
+            turn_y(m, n)
+        gather_y(0, n)
+        weigh(3, n)
+        for m in range(2, TILES):
+            turn_y(m, n)
+        gather_y(1, n)
+        quantise_y(0, n)
+        quantise_y(1, n)
+        store_y_scales(n, [nc.scalar, nc.sync])

@@ -50,32 +50,61 @@ def tile_polarisation_green_step_k6_kernel(
                 nc.scalar.copy(out=out, in_=in_)
 
         def case_rows(ap, m):
-            return ap.rearrange("(h i e) k -> h e i k", h=2, e=2)[m // 2, m % 2]
+            return ap[P * m : P * (m + 1), :]
 
         ident = sb("ident", [P, P], F32)
         make_identity(nc, ident[:])
 
+        warm_in = sb("warm_in", [P, W], BF16)
+        warm_codes = sb("warm_codes", [P, P], U32)
+        warm_scales = sb("warm_scales", [P, P], U8)
+        ebar_rows = sb("ebar_rows", [P, P], BF16)
+        ebar_wide = sb("ebar_wide", [P, P], F32)
+        nc.vector.memset(warm_in[:], 1.0)
+        nc.vector.memset(ebar_rows[:], 0.0)
         d_plane0 = sb("d_plane0", [P, C_PASSES, W], U8)
-        d_plane1 = sb("d_plane1", [P, C_PASSES, PTS - W], U8)
+        d_plane1 = sb("d_plane1", [P, C_PASSES, W], U8)
+        d_plane2 = sb("d_plane2", [P, C_PASSES, 2 * W], U8)
         g_plane = sb("g_plane", [P, N], U8)
         nc.vector.memset(d_plane0[:].rearrange("p j n -> p (j n)").bitcast(I32), 0)
+        nc.vector.quantize_mx(out=warm_codes[:].bitcast(FP8X4), scales=warm_scales[:], in_=warm_in[:])
+        warm_bank = new_bank()
+
+        def warm(count):
+            for unused in range(count):
+                nc.tensor.matmul_mx(
+                    out=warm_bank[:, :P],
+                    lhsT=warm_codes[:].bitcast(FP8X4),
+                    lhsT_scale=warm_scales[:],
+                    rhs=warm_codes[:].bitcast(FP8X4),
+                    rhs_scale=warm_scales[:],
+                    start=True,
+                    stop=True,
+                )
+
         nc.vector.memset(d_plane1[:].rearrange("p j n -> p (j n)").bitcast(I32), 0)
+        nc.vector.memset(d_plane2[:].rearrange("p j n -> p (j n)").bitcast(I32), 0)
         nc.vector.memset(g_plane[:].bitcast(I32), 0)
 
         con_rows = sb("con_rows", [P, PTS // P], BF16)
-        ebar_sb = sb("ebar_sb", [P, TILES], BF16)
+        ebar_sb = sb("ebar_sb", [P, TILES], F32)
         v_wide = sb("v_wide", [P, N], BF16)
         v_neg = sb("v_neg", [P, N], BF16)
         con_wide = sb("con_wide", [P, PTS], BF16)
-        a_sb = [sb("a%d" % m, [P, R], BF16) for m in range(TILES)]
+        a_sb = [sb("a%d" % h, [P, 2 * R], BF16) for h in range(2)]
         c_sb = [sb("c%d" % m, [P, Q], BF16) for m in range(TILES)]
         b_sb = [sb("b%d" % g, [P, 4, W], BF16) for g in range(PT_CHUNKS)]
         d_sb = [sb("d%d" % g, [P, C_PASSES, 2 * W], U8) for g in range(PT_CHUNKS)]
         g_sb = [sb("g%d" % n, [P, PT_CHUNKS, W], U32) for n in range(N_CHUNKS)]
 
-        def load_cases(m):
+        def load_c(m):
             nc.sync.dma_start(out=c_sb[m][:], in_=case_rows(c, m))
-            nc.sync.dma_start(out=a_sb[m][:], in_=case_rows(a, m))
+
+        def load_a(h):
+            nc.sync.dma_start(
+                out=a_sb[h][:].rearrange("i (e k) -> i e k", e=2),
+                in_=a[2 * P * h : 2 * P * (h + 1), :].rearrange("(e i) k -> i e k", e=2),
+            )
 
         def load_b(g):
             nc.sync.dma_start(out=b_sb[g][:], in_=b[:, W * g : W * (g + 1)].rearrange("(p t) n -> p t n", t=4))
@@ -93,23 +122,25 @@ def tile_polarisation_green_step_k6_kernel(
             src = gam_words.rearrange("g p n t -> p g (n t)")[:, :, 4 * W * n : 4 * W * (n + 1)]
             nc.sync.dma_start(out=g_sb[n][:].bitcast(I32), in_=src.bitcast(I32))
 
-        nc.sync.dma_start(out=con_rows[:], in_=contrast.rearrange("(p c) -> p c", p=P))
-        load_cases(0)
-        load_b(0)
+        nc.scalar.dma_start(out=con_rows[:], in_=contrast.rearrange("(p c) -> p c", p=P))
+        nc.scalar.dma_start(out=ebar_rows[:TILES, :], in_=ebar.rearrange("(m i) -> m i", m=TILES))
+        load_c(0)
+        load_a(0)
+        load_c(1)
         load_d_scales(nc.scalar, d_plane0, 0, W)
         load_d(0)
-        load_cases(1)
-        nc.sync.dma_start(
-            out=ebar_sb[:].rearrange("i (h e) -> i h e", h=2), in_=ebar.rearrange("(h i e) -> i h e", h=2, e=2)
-        )
-        load_cases(2)
-        load_cases(3)
+        load_c(2)
+        load_a(1)
+        load_b(0)
+        load_c(3)
         load_b(1)
-        load_d_scales(nc.sync, d_plane1, W, PTS)
+        load_d_scales(nc.sync, d_plane1, W, 2 * W)
         load_d(1)
-        for g in range(2, PT_CHUNKS):
-            load_b(g)
-            load_d(g)
+        load_b(2)
+        load_d_scales(nc.sync, d_plane2, 2 * W, PTS)
+        load_d(2)
+        load_b(3)
+        load_d(3)
         for q in range(4):
             nc.sync.dma_start(
                 out=g_plane[32 * q : 32 * q + 16, :].bitcast(I32),
@@ -120,7 +151,12 @@ def tile_polarisation_green_step_k6_kernel(
         load_gam(1)
         load_gam(2)
 
-        def spread_contrast():
+        def turn_ebar():
+            nc.vector.tensor_copy(out=ebar_wide[:], in_=ebar_rows[:])
+            nc.tensor.transpose(warm_bank[:, P : 2 * P], ebar_wide[:], ident[:])
+            nc.scalar.copy(out=ebar_sb[:], in_=warm_bank[:, P : P + TILES])
+
+        def spread_contrast(engines):
             words = con_rows[:].bitcast(F32)
             wide = con_wide[:].bitcast(F32).rearrange("j (g u r) -> j u g r", g=PT_CHUNKS, u=2)
             for u in range(2):
@@ -130,36 +166,62 @@ def tile_polarisation_green_step_k6_kernel(
                     nc.tensor.transpose(
                         bank[:, P * k : P * (k + 1)], words[:, col : col + 1].to_broadcast([P, P]), ident[:]
                     )
-                nc.scalar.copy(
-                    out=wide[:, u].rearrange("j g (r k) -> j g r k", k=4),
-                    in_=bank[:].rearrange("j (k g r) -> j g r k", k=4, g=PT_CHUNKS),
+                copy(
+                    engines[u],
+                    wide[:, u].rearrange("j g (r k) -> j g r k", k=4),
+                    bank[:].rearrange("j (k g r) -> j g r k", k=4, g=PT_CHUNKS),
                 )
 
         ac_codes = [sb("ac_codes%d" % m, [P, W], U32) for m in range(TILES)]
         ac_scales = [sb("ac_scales%d" % m, [P, W], U8) for m in range(TILES)]
         ac_grouped = {}
 
-        def turn_cases(m):
-            grouped = sb("ac_grouped", [P, 4 * W], BF16, bufs=2)
-            ac_grouped[m] = grouped
-            sources = [c_sb[m][:, W * j : W * (j + 1)] for j in range(C_PASSES)] + [a_sb[m][:]]
+        c_sorted = [sb("c_sorted%d" % m, [P, Q // 2], F32) for m in range(2)]
+        a_sorted = [sb("a_sorted%d" % h, [P, R], F32) for h in range(1)]
+
+        def sort_pairs(engine, out, in_):
+            copy(
+                engine,
+                out.rearrange("s (j u r i) -> s j r u i", u=2, r=32, i=4),
+                in_.bitcast(F32).rearrange("s (j r i u) -> s j r u i", u=2, r=32, i=4),
+            )
+
+        def sort_c(m, engine):
+            sort_pairs(engine, c_sorted[m][:], c_sb[m][:])
+
+        def sort_a(h, engine):
+            sort_pairs(engine, a_sorted[h][:], a_sb[h][:])
+
+        def turn_cases(m, engines):
+            if m < 2:
+                c_words, a_words = c_sorted[m][:], a_sorted[0][:]
+            else:
+                c_words, a_words = c_sb[m][:].bitcast(F32), a_sb[1][:].bitcast(F32)
+            sources = [c_words[:, 2 * P * j : 2 * P * (j + 1)] for j in range(C_PASSES)]
+            sources.append(a_words[:, 2 * P * (m % 2) : 2 * P * (m % 2 + 1)])
             for half in range(2):
                 bank = new_bank()
+                grouped = sb("ac_grouped%d" % half, [P, 2 * W], BF16, bufs=2)
+                ac_grouped[m, half] = grouped
                 for jj in range(2):
-                    words = sources[2 * half + jj].bitcast(F32)
+                    words = sources[2 * half + jj]
                     for u in range(2):
                         slot = 2 * jj + u
-                        nc.tensor.transpose(bank[:, P * slot : P * (slot + 1)], words[:, u : 2 * P : 2], ident[:])
-                nc.scalar.copy(
-                    out=grouped[:].bitcast(F32)[:, W * half : W * (half + 1)].rearrange("p (j i u) -> p j i u", j=2, u=2),
-                    in_=bank[:].rearrange("p (j u i) -> p j i u", j=2, u=2),
+                        pairs = words[:, P * u : P * (u + 1)] if m < 2 else words[:, u : 2 * P : 2]
+                        nc.tensor.transpose(bank[:, P * slot : P * (slot + 1)], pairs, ident[:])
+                copy(
+                    engines[half],
+                    grouped[:].bitcast(F32).rearrange("p (j i u) -> p j i u", j=2, u=2),
+                    bank[:].rearrange("p (j u i) -> p j i u", j=2, u=2),
                 )
 
         def quantise(codes, scales, grouped):
             nc.vector.quantize_mx(out=codes.bitcast(FP8X4), scales=scales, in_=grouped)
 
         def quantise_cases(m):
-            quantise(ac_codes[m][:], ac_scales[m][:], ac_grouped[m][:])
+            for half in range(2):
+                cols = slice(2 * P * half, 2 * P * (half + 1))
+                quantise(ac_codes[m][:, cols], ac_scales[m][:, cols], ac_grouped[m, half][:])
 
         b_codes = [sb("b_codes%d" % g, [P, W], U32) for g in range(PT_CHUNKS)]
         b_scales = [sb("b_scales%d" % g, [P, W], U8) for g in range(PT_CHUNKS)]
@@ -181,17 +243,20 @@ def tile_polarisation_green_step_k6_kernel(
 
         strain_bank = {}
 
-        def strain_matmuls(m, g):
-            bank = new_bank()
-            strain_bank[m, g] = bank
-            for j in range(C_PASSES + 1):
+        def strain_matmuls(m, g, passes=(0, 1, 2, 3)):
+            if passes[0] == 0:
+                strain_bank[m, g] = new_bank()
+            bank = strain_bank[m, g]
+            for j in passes:
                 cols = slice(P * j, P * (j + 1))
                 if j == C_PASSES:
                     rhs, rhs_scale = b_codes[g][:].bitcast(FP8X4), b_scales[g][:]
                 elif g == 0:
                     rhs, rhs_scale = d_sb[g][:, j, :].bitcast(FP4X4), d_plane0[:, j, :]
+                elif g == 1:
+                    rhs, rhs_scale = d_sb[g][:, j, :].bitcast(FP4X4), d_plane1[:, j, :]
                 else:
-                    rhs, rhs_scale = d_sb[g][:, j, :].bitcast(FP4X4), d_plane1[:, j, W * (g - 1) : W * g]
+                    rhs, rhs_scale = d_sb[g][:, j, :].bitcast(FP4X4), d_plane2[:, j, W * (g - 2) : W * (g - 1)]
                 nc.tensor.matmul_mx(
                     out=bank[:],
                     lhsT=ac_codes[m][:, cols].bitcast(FP8X4),
@@ -208,7 +273,7 @@ def tile_polarisation_green_step_k6_kernel(
         tau_sb = {}
 
         def polarise(m, g):
-            tau = sb("tau%d" % m, [P, W], BF16, bufs=2)
+            tau = sb("tau%d" % m, [P, W], BF16, bufs=3)
             tau_sb[m, g] = tau
             for u in range(2):
                 half = slice(W * g + 2 * P * u, W * g + 2 * P * (u + 1))
@@ -284,44 +349,37 @@ def tile_polarisation_green_step_k6_kernel(
             rounded = sb("y_half%d" % m, [P, W], BF16, bufs=2)
             y_half[m, n] = rounded
             nc.scalar.copy(
-                out=rounded[:].rearrange("s (u p e) -> s u p e", u=2, e=2),
-                in_=y_sb[m, n][:].rearrange("s (p u e) -> s u p e", u=2, e=2),
+                out=rounded[:].rearrange("s (u r i e) -> s r u i e", u=2, i=4, e=2),
+                in_=y_sb[m, n][:].rearrange("s (r i u e) -> s r u i e", u=2, i=4, e=2),
             )
-
-        def weigh_rounded(m, n):
-            rounded = sb("y_half%d" % m, [P, W], BF16, bufs=2)
-            y_half[m, n] = rounded
-            for u in range(2):
-                nc.vector.scalar_tensor_tensor(
-                    out=rounded[:, 2 * P * u : 2 * P * (u + 1)].rearrange("s (p e) -> s p e", e=2),
-                    in0=sorted_pairs(green_bank[m, n][:], u),
-                    scalar=ebar_sb[:, m : m + 1],
-                    in1=sorted_pairs(v_neg[:, W * n : W * (n + 1)], u),
-                    op0=ALU.subtract,
-                    op1=ALU.mult,
-                )
 
         y_codes = [sb("y_codes%d" % n, [P, W], U32) for n in range(N_CHUNKS)]
         y_scales = [sb("y_scales%d" % n, [P, W], U8) for n in range(N_CHUNKS)]
-        y_bank = {}
+        y_turned = {}
         y_grouped = {}
 
-        def turn_y(m, n):
-            if m % 2 == 0:
-                y_bank[m // 2, n] = new_bank()
-            turn_tile(y_bank[m // 2, n], m % 2, y_half[m, n])
+        def turn_y(n, tiles):
+            bank = new_bank()
+            y_turned[n, tiles[0]] = bank
+            for e, m in enumerate(tiles):
+                turn_tile(bank, e, y_half[m, n])
 
-        def gather_y(h, n):
-            grouped = sb("y_grouped%d" % h, [P, 2 * W], BF16, bufs=2)
-            y_grouped[h, n] = grouped
-            nc.scalar.copy(
-                out=grouped[:].bitcast(F32).rearrange("p (i e u) -> p i e u", e=2, u=2),
-                in_=y_bank[h, n][:].rearrange("p (e u i) -> p i e u", e=2, u=2),
+        def gather_y(n, tiles, engine):
+            width = 2 * P * len(tiles)
+            grouped = sb("y_grouped%d" % len(tiles), [P, 2 * width], BF16, bufs=2)
+            y_grouped[n, tiles[0]] = grouped
+            copy(
+                engine,
+                grouped[:].bitcast(F32).rearrange("p (e i u) -> p e i u", i=P, u=2),
+                y_turned[n, tiles[0]][:, :width].rearrange("p (e u i) -> p e i u", i=P, u=2),
             )
 
-        def quantise_y(h, n):
-            cols = slice(2 * P * h, 2 * P * (h + 1))
-            quantise(y_codes[n][:, cols], y_scales[n][:, cols], y_grouped[h, n][:])
+        def quantise_y(n, tiles):
+            cols = slice(P * tiles[0], P * (tiles[-1] + 1))
+            quantise(y_codes[n][:, cols], y_scales[n][:, cols], y_grouped[n, tiles[0]][:])
+
+        def store_y_words(n, tiles):
+            cols = slice(P * tiles[0], P * (tiles[-1] + 1))
             nc.sync.dma_start(
                 out=out_1[n].rearrange("p m t -> p (m t)").bitcast(I32)[:, cols], in_=y_codes[n][:, cols].bitcast(I32)
             )
@@ -332,100 +390,143 @@ def tile_polarisation_green_step_k6_kernel(
                     out=out_2[n, 4 * q : 4 * q + 4, :].bitcast(I32), in_=y_scales[n][32 * q : 32 * q + 4, :].bitcast(I32)
                 )
 
-        spread_contrast()
-        turn_cases(0)
-        interleave_b(0, ["vector"])
+        def last_half(m, n, k, y, rounded):
+            bank = new_bank()
+            cols = slice(P * m, P * (m + 1))
+            part = slice(2 * P * k, 2 * P * (k + 1))
+            whole = slice(W * n + 2 * P * k, W * n + 2 * P * (k + 1))
+            for g in range(PT_CHUNKS):
+                nc.tensor.matmul_mx(
+                    out=bank[:, : 2 * P],
+                    lhsT=tau_codes[g][:, cols].bitcast(FP8X4),
+                    lhsT_scale=tau_scales[g][:, cols],
+                    rhs=g_sb[n][:, g, part].bitcast(FP8X4),
+                    rhs_scale=g_plane[4 * g :, whole],
+                    start=(g == 0),
+                    stop=(g == PT_CHUNKS - 1),
+                )
+            for u in range(2):
+                nc.vector.scalar_tensor_tensor(
+                    out=rounded[:, 2 * P * u + P * k : 2 * P * u + P * (k + 1)].rearrange("s (p e) -> s p e", e=2),
+                    in0=sorted_pairs(bank[:, : 2 * P], u),
+                    scalar=ebar_sb[:, m : m + 1],
+                    in1=sorted_pairs(v_neg[:, whole], u),
+                    op0=ALU.subtract,
+                    op1=ALU.mult,
+                )
+            nc.vector.scalar_tensor_tensor(
+                out=y[:, part],
+                in0=bank[:, : 2 * P],
+                scalar=ebar_sb[:, m : m + 1],
+                in1=v_neg[:, whole],
+                op0=ALU.subtract,
+                op1=ALU.mult,
+            )
+
+        warm(14)
+        turn_ebar()
+        sort_c(0, "vector")
+        sort_a(0, "vector")
+        turn_cases(0, ["scalar", "scalar"])
+        warm(6)
+        sort_c(1, "vector")
         quantise_cases(0)
-        quantise_b(0)
-        turn_cases(1)
+        turn_cases(1, ["scalar", "vector"])
         quantise_cases(1)
-        strain_matmuls(0, 0)
-        turn_cases(2)
-        polarise(0, 0)
+        spread_contrast(["scalar", "scalar"])
+        strain_matmuls(0, 0, (0, 1, 2))
+        turn_cases(2, ["scalar", "scalar"])
         quantise_cases(2)
-        strain_matmuls(1, 0)
-        turn_cases(3)
-        polarise(1, 0)
+        strain_matmuls(1, 0, (0, 1, 2))
+        strain_matmuls(2, 0, (0, 1, 2))
+        interleave_b(0, ["vector", "scalar"])
+        quantise_b(0)
+        turn_cases(3, ["scalar", "scalar"])
         quantise_cases(3)
+        strain_matmuls(0, 0, (3,))
+        strain_matmuls(1, 0, (3,))
+        strain_matmuls(2, 0, (3,))
+        polarise(0, 0)
         interleave_b(1, ["vector", "scalar"])
-        strain_matmuls(2, 0)
-        polarise(2, 0)
-        quantise_b(1)
         strain_matmuls(3, 0)
+        quantise_b(1)
+        polarise(1, 0)
+        polarise(2, 0)
         polarise(3, 0)
 
         for g in range(1, PT_CHUNKS):
             more = g + 1 < PT_CHUNKS
+            turned = [0, 1] if g == 2 else []
             if more:
                 interleave_b(g + 1, ["scalar"])
-            strain_matmuls(0, g)
-            polarise(0, g)
-            strain_matmuls(1, g)
-            polarise(1, g)
-            turn_tau(g - 1, 0, "scalar")
-            turn_tau(g - 1, 1, "scalar")
+            for m in range(2):
+                strain_matmuls(m, g, (0, 1, 2))
+            for m in range(2):
+                strain_matmuls(m, g, (3,))
+                polarise(m, g)
+            for done in turned:
+                for h in range(2):
+                    turn_tau(done, h, "scalar")
             if more:
                 quantise_b(g + 1)
             else:
                 nc.vector.tensor_scalar(out=v_neg[:], in0=v_wide[:], scalar1=-1.0, scalar2=None, op0=ALU.mult)
-            strain_matmuls(2, g)
-            quantise_tau(g - 1, 0)
-            polarise(2, g)
-            quantise_tau(g - 1, 1)
-            strain_matmuls(3, g)
-            polarise(3, g)
+            for m in range(2, TILES):
+                strain_matmuls(m, g)
+                polarise(m, g)
+            for done in turned:
+                for h in range(2):
+                    quantise_tau(done, h)
 
-        last = PT_CHUNKS - 1
-        early = list(range(last))
-        green_matmuls(0, 0, early)
-        green_matmuls(1, 0, early)
-        turn_tau(last, 0, "scalar")
-        turn_tau(last, 1, "vector")
-        quantise_tau(last, 0)
-        quantise_tau(last, 1)
-        green_matmuls(2, 0, early)
-        for m in range(2):
-            green_matmuls(m, 0, [last])
-        for m in range(2):
-            weigh(m, 0)
-            round_y(m, 0)
-        green_matmuls(3, 0, early)
-        for m in range(2, TILES):
-            green_matmuls(m, 0, [last])
-        for m in range(2, TILES):
+        green_matmuls(0, 0, [0, 1])
+        for done in (2, 3):
+            for h in range(2):
+                turn_tau(done, h, "scalar" if h == 0 else "vector")
+            for h in range(2):
+                quantise_tau(done, h)
+        for m in range(1, TILES):
+            green_matmuls(m, 0, [0, 1])
+        for m in range(TILES):
+            green_matmuls(m, 0, [2, 3])
             weigh(m, 0)
             round_y(m, 0)
 
         every = list(range(PT_CHUNKS))
+        last = N_CHUNKS - 1
         for n in range(1, N_CHUNKS):
-            for m in range(2):
+            green_matmuls(0, n, every)
+            weigh(0, n)
+            for pair in ([0, 1], [2, 3]):
+                turn_y(n - 1, pair)
+                gather_y(n - 1, pair, "scalar")
+            round_y(0, n)
+            green_matmuls(1, n, every)
+            quantise_y(n - 1, [0, 1])
+            weigh(1, n)
+            round_y(1, n)
+            quantise_y(n - 1, [2, 3])
+            store_y_words(n - 1, [0, 1, 2, 3])
+            store_y_scales(n - 1, [nc.sync])
+            for m in range(2, TILES if n < last else TILES - 1):
                 green_matmuls(m, n, every)
                 weigh(m, n)
                 round_y(m, n)
-            for m in range(TILES):
-                turn_y(m, n - 1)
-            for h in range(2):
-                gather_y(h, n - 1)
-            green_matmuls(2, n, every)
-            quantise_y(0, n - 1)
-            weigh(2, n)
-            round_y(2, n)
-            quantise_y(1, n - 1)
-            store_y_scales(n - 1, [nc.sync])
-            green_matmuls(3, n, every)
-            if n + 1 < N_CHUNKS:
-                weigh(3, n)
-                round_y(3, n)
 
-        n = N_CHUNKS - 1
-        weigh_rounded(3, n)
-        for m in range(2):
-            turn_y(m, n)
-        gather_y(0, n)
-        weigh(3, n)
-        for m in range(2, TILES):
-            turn_y(m, n)
-        gather_y(1, n)
-        quantise_y(0, n)
-        quantise_y(1, n)
-        store_y_scales(n, [nc.scalar, nc.sync])
+        y = sb("y3", [P, W], F32, bufs=2)
+        rounded = sb("y_half3", [P, W], BF16, bufs=2)
+        y_half[3, last] = rounded
+        for k in range(2):
+            last_half(3, last, k, y, rounded)
+        nc.sync.dma_start(out=case_rows(out_0, 3)[:, W * last :], in_=y[:])
+        turn_y(last, [0, 1])
+        gather_y(last, [0, 1], "scalar")
+        turn_y(last, [2])
+        gather_y(last, [2], "scalar")
+        turn_y(last, [3])
+        gather_y(last, [3], "vector")
+        quantise_y(last, [0, 1])
+        store_y_words(last, [0, 1])
+        quantise_y(last, [2])
+        quantise_y(last, [3])
+        store_y_words(last, [2, 3])
+        store_y_scales(last, [nc.scalar, nc.sync])

@@ -19,6 +19,7 @@ P = 128
 W = 512
 TILES = 4
 BANKS = 8
+AHEAD = 3
 C_PASSES = Q // W
 PT_CHUNKS = PTS // W
 N_CHUNKS = N // W
@@ -33,15 +34,20 @@ def tile_polarisation_green_step_k6_kernel(
         psum = ctx.enter_context(tc.psum_pool(name="psum", bufs=1))
         ctx.enter_context(tc.manual_schedule())
 
-        taken = []
+        free_banks = list(range(BANKS))
+        bank_index = {}
 
-        def new_bank():
-            index = len(taken) % BANKS
-            taken.append(index)
+        def new_bank(key):
+            index = free_banks[0]
+            free_banks.remove(index)
+            bank_index[key] = index
             return psum.tile([P, W], F32, name="bank%d" % index)
 
+        def release(key):
+            free_banks.append(bank_index[key])
+
         def sb(name, shape, dtype, bufs=1):
-            return keep.tile(shape, dtype, name=name, bufs=bufs, align_bytes=64)
+            return keep.tile(shape, dtype, name=name, bufs=bufs, align_bytes=256)
 
         def copy(engine, out, in_):
             if engine == "vector":
@@ -68,7 +74,7 @@ def tile_polarisation_green_step_k6_kernel(
         g_plane = sb("g_plane", [P, N], U8)
         nc.vector.memset(d_plane0[:].rearrange("p j n -> p (j n)").bitcast(I32), 0)
         nc.vector.quantize_mx(out=warm_codes[:].bitcast(FP8X4), scales=warm_scales[:], in_=warm_in[:])
-        warm_bank = new_bank()
+        warm_bank = new_bank("warm")
 
         def warm(count):
             for unused in range(count):
@@ -88,10 +94,10 @@ def tile_polarisation_green_step_k6_kernel(
 
         con_rows = sb("con_rows", [P, PTS // P], BF16)
         ebar_sb = sb("ebar_sb", [P, TILES], F32)
-        v_wide = sb("v_wide", [P, N], BF16)
-        v_neg = sb("v_neg", [P, N], BF16)
-        con_wide = sb("con_wide", [P, PTS], BF16)
-        a_sb = [sb("a%d" % h, [P, 2 * R], BF16) for h in range(2)]
+        v_wide = [sb("v_wide%d" % n, [P, W], BF16) for n in range(N_CHUNKS)]
+        v_neg = [sb("v_neg%d" % n, [P, W], BF16) for n in range(N_CHUNKS)]
+        con_wide = [sb("con_wide%d" % u, [P, PTS // 2], BF16) for u in range(2)]
+        a_sb = sb("a_sb", [P, TILES * R], BF16)
         c_sb = [sb("c%d" % m, [P, Q], BF16) for m in range(TILES)]
         b_sb = [sb("b%d" % g, [P, 4, W], BF16) for g in range(PT_CHUNKS)]
         d_sb = [sb("d%d" % g, [P, C_PASSES, 2 * W], U8) for g in range(PT_CHUNKS)]
@@ -100,10 +106,9 @@ def tile_polarisation_green_step_k6_kernel(
         def load_c(m):
             nc.sync.dma_start(out=c_sb[m][:], in_=case_rows(c, m))
 
-        def load_a(h):
+        def load_a():
             nc.sync.dma_start(
-                out=a_sb[h][:].rearrange("i (e k) -> i e k", e=2),
-                in_=a[2 * P * h : 2 * P * (h + 1), :].rearrange("(e i) k -> i e k", e=2),
+                out=a_sb[:].rearrange("i (m k) -> i m k", m=TILES), in_=a.rearrange("(m i) k -> i m k", m=TILES)
             )
 
         def load_b(g):
@@ -114,9 +119,9 @@ def tile_polarisation_green_step_k6_kernel(
             nc.sync.dma_start(out=d_sb[g][:].bitcast(I32), in_=src.bitcast(I32))
 
         def load_d_scales(queue, plane, first, last):
-            for q in range(4):
-                src = d_scales[:, 4 * q : 4 * q + 4, first:last].rearrange("j r n -> r j n")
-                queue.dma_start(out=plane[32 * q : 32 * q + 4, :, :].bitcast(I32), in_=src.bitcast(I32))
+            for r in range(4):
+                src = d_scales[:, r:16:4, first:last].rearrange("j q n -> q j n")
+                queue.dma_start(out=plane[r:P:32, :, :].bitcast(I32), in_=src.bitcast(I32))
 
         def load_gam(n):
             src = gam_words.rearrange("g p n t -> p g (n t)")[:, :, 4 * W * n : 4 * W * (n + 1)]
@@ -125,17 +130,16 @@ def tile_polarisation_green_step_k6_kernel(
         nc.scalar.dma_start(out=con_rows[:], in_=contrast.rearrange("(p c) -> p c", p=P))
         nc.scalar.dma_start(out=ebar_rows[:TILES, :], in_=ebar.rearrange("(m i) -> m i", m=TILES))
         load_c(0)
-        load_a(0)
         load_c(1)
         load_d_scales(nc.scalar, d_plane0, 0, W)
         load_d(0)
         load_c(2)
-        load_a(1)
-        load_b(0)
         load_c(3)
-        load_b(1)
+        load_a()
+        load_b(0)
         load_d_scales(nc.sync, d_plane1, W, 2 * W)
         load_d(1)
+        load_b(1)
         load_b(2)
         load_d_scales(nc.sync, d_plane2, 2 * W, PTS)
         load_d(2)
@@ -146,21 +150,19 @@ def tile_polarisation_green_step_k6_kernel(
                 out=g_plane[32 * q : 32 * q + 16, :].bitcast(I32),
                 in_=gam_scales[:, 4 * q : 4 * q + 4, :].bitcast(I32),
             )
-        load_gam(0)
-        nc.sync.dma_start(out=v_wide[:], in_=v.partition_broadcast(P))
-        load_gam(1)
-        load_gam(2)
+        for n in range(N_CHUNKS):
+            load_gam(n)
+            nc.sync.dma_start(out=v_wide[n][:], in_=v[W * n : W * (n + 1)].partition_broadcast(P))
 
         def turn_ebar():
-            nc.vector.tensor_copy(out=ebar_wide[:], in_=ebar_rows[:])
             nc.tensor.transpose(warm_bank[:, P : 2 * P], ebar_wide[:], ident[:])
             nc.scalar.copy(out=ebar_sb[:], in_=warm_bank[:, P : P + TILES])
+            release("warm")
 
         def spread_contrast(engines):
             words = con_rows[:].bitcast(F32)
-            wide = con_wide[:].bitcast(F32).rearrange("j (g u r) -> j u g r", g=PT_CHUNKS, u=2)
             for u in range(2):
-                bank = new_bank()
+                bank = new_bank("contrast")
                 for k in range(4):
                     col = 2 * k + u
                     nc.tensor.transpose(
@@ -168,60 +170,60 @@ def tile_polarisation_green_step_k6_kernel(
                     )
                 copy(
                     engines[u],
-                    wide[:, u].rearrange("j g (r k) -> j g r k", k=4),
-                    bank[:].rearrange("j (k g r) -> j g r k", k=4, g=PT_CHUNKS),
+                    con_wide[u][:].bitcast(F32).rearrange("j (r k) -> j r k", k=4),
+                    bank[:].rearrange("j (k r) -> j r k", k=4),
                 )
+                release("contrast")
 
-        ac_codes = [sb("ac_codes%d" % m, [P, W], U32) for m in range(TILES)]
-        ac_scales = [sb("ac_scales%d" % m, [P, W], U8) for m in range(TILES)]
+        sets = []
+        for m in range(TILES):
+            sets.extend([[(m, 0), (m, 1)], [(m, 2)]])
+        sets.extend([[(0, 3), (1, 3)], [(2, 3), (3, 3)]])
+        place = {unit: (k, side) for k, units in enumerate(sets) for side, unit in enumerate(units)}
+        ac_codes = [sb("ac_codes%d" % k, [P, P * len(units)], U32) for k, units in enumerate(sets)]
+        ac_scales = [sb("ac_scales%d" % k, [P, P * len(units)], U8) for k, units in enumerate(sets)]
+        ac_bank = {}
         ac_grouped = {}
 
-        c_sorted = [sb("c_sorted%d" % m, [P, Q // 2], F32) for m in range(2)]
-        a_sorted = [sb("a_sorted%d" % h, [P, R], F32) for h in range(1)]
+        c_sorted = sb("c_sorted", [P, Q // 2], F32)
+        a_sorted = sb("a_sorted", [P, TILES * R // 2], F32)
 
-        def sort_pairs(engine, out, in_):
-            copy(
-                engine,
-                out.rearrange("s (j u r i) -> s j r u i", u=2, r=32, i=4),
-                in_.bitcast(F32).rearrange("s (j r i u) -> s j r u i", u=2, r=32, i=4),
+        def sort_words(out, in_):
+            nc.vector.tensor_copy(
+                out=out.rearrange("s (j u r i) -> s j r u i", u=2, r=32, i=4),
+                in_=in_.bitcast(F32).rearrange("s (j r i u) -> s j r u i", u=2, r=32, i=4),
             )
 
-        def sort_c(m, engine):
-            sort_pairs(engine, c_sorted[m][:], c_sb[m][:])
+        def unit_words(m, j, u):
+            if j == C_PASSES:
+                return a_sorted[:, 2 * P * m + P * u : 2 * P * m + P * (u + 1)]
+            if m == TILES - 1:
+                return c_sorted[:, 2 * P * j + P * u : 2 * P * j + P * (u + 1)]
+            return c_sb[m][:].bitcast(F32)[:, 2 * P * j + u : 2 * P * (j + 1) : 2]
 
-        def sort_a(h, engine):
-            sort_pairs(engine, a_sorted[h][:], a_sb[h][:])
+        def turn_set(k):
+            ac_bank[k] = new_bank(("cases", k))
+            for side, (m, j) in enumerate(sets[k]):
+                for u in range(2):
+                    slot = 2 * side + u
+                    nc.tensor.transpose(ac_bank[k][:, P * slot : P * (slot + 1)], unit_words(m, j, u), ident[:])
 
-        def turn_cases(m, engines):
-            if m < 2:
-                c_words, a_words = c_sorted[m][:], a_sorted[0][:]
-            else:
-                c_words, a_words = c_sb[m][:].bitcast(F32), a_sb[1][:].bitcast(F32)
-            sources = [c_words[:, 2 * P * j : 2 * P * (j + 1)] for j in range(C_PASSES)]
-            sources.append(a_words[:, 2 * P * (m % 2) : 2 * P * (m % 2 + 1)])
-            for half in range(2):
-                bank = new_bank()
-                grouped = sb("ac_grouped%d" % half, [P, 2 * W], BF16, bufs=2)
-                ac_grouped[m, half] = grouped
-                for jj in range(2):
-                    words = sources[2 * half + jj]
-                    for u in range(2):
-                        slot = 2 * jj + u
-                        pairs = words[:, P * u : P * (u + 1)] if m < 2 else words[:, u : 2 * P : 2]
-                        nc.tensor.transpose(bank[:, P * slot : P * (slot + 1)], pairs, ident[:])
-                copy(
-                    engines[half],
-                    grouped[:].bitcast(F32).rearrange("p (j i u) -> p j i u", j=2, u=2),
-                    bank[:].rearrange("p (j u i) -> p j i u", j=2, u=2),
-                )
+        def gather_set(k, engine):
+            count = len(sets[k])
+            grouped = sb("ac_grouped%d" % count, [P, W * count], BF16, bufs=3)
+            ac_grouped[k] = grouped
+            copy(
+                engine,
+                grouped[:].bitcast(F32).rearrange("p (j i u) -> p j i u", i=P, u=2),
+                ac_bank[k][:, : 2 * P * count].rearrange("p (j u i) -> p j i u", i=P, u=2),
+            )
+            release(("cases", k))
 
         def quantise(codes, scales, grouped):
             nc.vector.quantize_mx(out=codes.bitcast(FP8X4), scales=scales, in_=grouped)
 
-        def quantise_cases(m):
-            for half in range(2):
-                cols = slice(2 * P * half, 2 * P * (half + 1))
-                quantise(ac_codes[m][:, cols], ac_scales[m][:, cols], ac_grouped[m, half][:])
+        def quantise_set(k):
+            quantise(ac_codes[k][:], ac_scales[k][:], ac_grouped[k][:])
 
         b_codes = [sb("b_codes%d" % g, [P, W], U32) for g in range(PT_CHUNKS)]
         b_scales = [sb("b_scales%d" % g, [P, W], U8) for g in range(PT_CHUNKS)]
@@ -245,10 +247,11 @@ def tile_polarisation_green_step_k6_kernel(
 
         def strain_matmuls(m, g, passes=(0, 1, 2, 3)):
             if passes[0] == 0:
-                strain_bank[m, g] = new_bank()
+                strain_bank[m, g] = new_bank(("strain", m, g))
             bank = strain_bank[m, g]
             for j in passes:
-                cols = slice(P * j, P * (j + 1))
+                k, side = place[m, j]
+                cols = slice(P * side, P * (side + 1))
                 if j == C_PASSES:
                     rhs, rhs_scale = b_codes[g][:].bitcast(FP8X4), b_scales[g][:]
                 elif g == 0:
@@ -259,8 +262,8 @@ def tile_polarisation_green_step_k6_kernel(
                     rhs, rhs_scale = d_sb[g][:, j, :].bitcast(FP4X4), d_plane2[:, j, W * (g - 2) : W * (g - 1)]
                 nc.tensor.matmul_mx(
                     out=bank[:],
-                    lhsT=ac_codes[m][:, cols].bitcast(FP8X4),
-                    lhsT_scale=ac_scales[m][:, cols],
+                    lhsT=ac_codes[k][:, cols].bitcast(FP8X4),
+                    lhsT_scale=ac_scales[k][:, cols],
                     rhs=rhs,
                     rhs_scale=rhs_scale,
                     start=(j == 0),
@@ -276,15 +279,16 @@ def tile_polarisation_green_step_k6_kernel(
             tau = sb("tau%d" % m, [P, W], BF16, bufs=3)
             tau_sb[m, g] = tau
             for u in range(2):
-                half = slice(W * g + 2 * P * u, W * g + 2 * P * (u + 1))
+                half = slice(2 * P * g, 2 * P * (g + 1))
                 nc.vector.scalar_tensor_tensor(
                     out=tau[:, 2 * P * u : 2 * P * (u + 1)].rearrange("s (p e) -> s p e", e=2),
                     in0=sorted_pairs(strain_bank[m, g][:], u),
                     scalar=ebar_sb[:, m : m + 1],
-                    in1=con_wide[:, half].rearrange("s (p e) -> s p e", e=2),
+                    in1=con_wide[u][:, half].rearrange("s (p e) -> s p e", e=2),
                     op0=ALU.add,
                     op1=ALU.mult,
                 )
+            release(("strain", m, g))
 
         def turn_tile(bank, e, source):
             words = source[:].bitcast(F32)
@@ -297,7 +301,7 @@ def tile_polarisation_green_step_k6_kernel(
         tau_grouped = {}
 
         def turn_tau(g, h, engine):
-            bank = new_bank()
+            bank = new_bank("tau")
             for e in range(2):
                 turn_tile(bank, e, tau_sb[2 * h + e, g])
             grouped = sb("tau_grouped%d" % h, [P, 2 * W], BF16, bufs=2)
@@ -307,6 +311,7 @@ def tile_polarisation_green_step_k6_kernel(
                 grouped[:].bitcast(F32).rearrange("p (e i u) -> p e i u", e=2, u=2),
                 bank[:].rearrange("p (e u i) -> p e i u", e=2, u=2),
             )
+            release("tau")
 
         def quantise_tau(g, h):
             cols = slice(2 * P * h, 2 * P * (h + 1))
@@ -316,7 +321,7 @@ def tile_polarisation_green_step_k6_kernel(
 
         def green_matmuls(m, n, passes):
             if passes[0] == 0:
-                green_bank[m, n] = new_bank()
+                green_bank[m, n] = new_bank(("green", m, n))
             cols = slice(P * m, P * (m + 1))
             for g in passes:
                 nc.tensor.matmul_mx(
@@ -329,6 +334,9 @@ def tile_polarisation_green_step_k6_kernel(
                     stop=(g == PT_CHUNKS - 1),
                 )
 
+        def negate_v(n):
+            nc.vector.tensor_scalar(out=v_neg[n][:], in0=v_wide[n][:], scalar1=-1.0, scalar2=None, op0=ALU.mult)
+
         y_sb = {}
         y_half = {}
 
@@ -339,10 +347,11 @@ def tile_polarisation_green_step_k6_kernel(
                 out=y[:],
                 in0=green_bank[m, n][:],
                 scalar=ebar_sb[:, m : m + 1],
-                in1=v_neg[:, W * n : W * (n + 1)],
+                in1=v_neg[n][:],
                 op0=ALU.subtract,
                 op1=ALU.mult,
             )
+            release(("green", m, n))
             nc.sync.dma_start(out=case_rows(out_0, m)[:, W * n : W * (n + 1)], in_=y[:])
 
         def round_y(m, n):
@@ -354,12 +363,12 @@ def tile_polarisation_green_step_k6_kernel(
             )
 
         y_codes = [sb("y_codes%d" % n, [P, W], U32) for n in range(N_CHUNKS)]
-        y_scales = [sb("y_scales%d" % n, [P, W], U8) for n in range(N_CHUNKS)]
+        y_scales = sb("y_scales", [P, N], U8)
         y_turned = {}
         y_grouped = {}
 
         def turn_y(n, tiles):
-            bank = new_bank()
+            bank = new_bank(("y", n, tiles[0]))
             y_turned[n, tiles[0]] = bank
             for e, m in enumerate(tiles):
                 turn_tile(bank, e, y_half[m, n])
@@ -373,10 +382,12 @@ def tile_polarisation_green_step_k6_kernel(
                 grouped[:].bitcast(F32).rearrange("p (e i u) -> p e i u", i=P, u=2),
                 y_turned[n, tiles[0]][:, :width].rearrange("p (e u i) -> p e i u", i=P, u=2),
             )
+            release(("y", n, tiles[0]))
 
         def quantise_y(n, tiles):
             cols = slice(P * tiles[0], P * (tiles[-1] + 1))
-            quantise(y_codes[n][:, cols], y_scales[n][:, cols], y_grouped[n, tiles[0]][:])
+            plane = y_scales[:, W * n : W * (n + 1)]
+            quantise(y_codes[n][:, cols], plane[:, cols], y_grouped[n, tiles[0]][:])
 
         def store_y_words(n, tiles):
             cols = slice(P * tiles[0], P * (tiles[-1] + 1))
@@ -384,72 +395,109 @@ def tile_polarisation_green_step_k6_kernel(
                 out=out_1[n].rearrange("p m t -> p (m t)").bitcast(I32)[:, cols], in_=y_codes[n][:, cols].bitcast(I32)
             )
 
-        def store_y_scales(n, queues):
-            for q in range(4):
-                queues[q % len(queues)].dma_start(
-                    out=out_2[n, 4 * q : 4 * q + 4, :].bitcast(I32), in_=y_scales[n][32 * q : 32 * q + 4, :].bitcast(I32)
+        def store_y_scales(first, count, queues):
+            for r in range(4):
+                rows = y_scales[r:P:32, W * first : W * (first + count)]
+                queues[r % len(queues)].dma_start(
+                    out=out_2[first : first + count, r:16:4, :].rearrange("n q m -> q n m").bitcast(I32),
+                    in_=rows.rearrange("q (n m) -> q n m", m=W).bitcast(I32),
                 )
 
-        def last_half(m, n, k, y, rounded):
-            bank = new_bank()
+        def finish_chunk(n):
+            quantise_y(n, [2, 3])
+            store_y_words(n, [0, 1, 2, 3])
+
+        half_bank = {}
+
+        def green_half(m, n, k):
+            bank = new_bank(("half", k))
+            half_bank[k] = bank
             cols = slice(P * m, P * (m + 1))
-            part = slice(2 * P * k, 2 * P * (k + 1))
-            whole = slice(W * n + 2 * P * k, W * n + 2 * P * (k + 1))
             for g in range(PT_CHUNKS):
                 nc.tensor.matmul_mx(
                     out=bank[:, : 2 * P],
                     lhsT=tau_codes[g][:, cols].bitcast(FP8X4),
                     lhsT_scale=tau_scales[g][:, cols],
-                    rhs=g_sb[n][:, g, part].bitcast(FP8X4),
-                    rhs_scale=g_plane[4 * g :, whole],
+                    rhs=g_sb[n][:, g, 2 * P * k : 2 * P * (k + 1)].bitcast(FP8X4),
+                    rhs_scale=g_plane[4 * g :, W * n + 2 * P * k : W * n + 2 * P * (k + 1)],
                     start=(g == 0),
                     stop=(g == PT_CHUNKS - 1),
                 )
+
+        def weigh_half_rounded(m, n, k):
             for u in range(2):
                 nc.vector.scalar_tensor_tensor(
-                    out=rounded[:, 2 * P * u + P * k : 2 * P * u + P * (k + 1)].rearrange("s (p e) -> s p e", e=2),
-                    in0=sorted_pairs(bank[:, : 2 * P], u),
+                    out=y_half[m, n][:, 2 * P * u + P * k : 2 * P * u + P * (k + 1)].rearrange("s (p e) -> s p e", e=2),
+                    in0=sorted_pairs(half_bank[k][:, : 2 * P], u),
                     scalar=ebar_sb[:, m : m + 1],
-                    in1=sorted_pairs(v_neg[:, whole], u),
+                    in1=sorted_pairs(v_neg[n][:, 2 * P * k : 2 * P * (k + 1)], u),
                     op0=ALU.subtract,
                     op1=ALU.mult,
                 )
+
+        def weigh_half(m, n, k):
+            part = slice(2 * P * k, 2 * P * (k + 1))
             nc.vector.scalar_tensor_tensor(
-                out=y[:, part],
-                in0=bank[:, : 2 * P],
+                out=y_sb[m, n][:, part],
+                in0=half_bank[k][:, : 2 * P],
                 scalar=ebar_sb[:, m : m + 1],
-                in1=v_neg[:, whole],
+                in1=v_neg[n][:, part],
                 op0=ALU.subtract,
                 op1=ALU.mult,
             )
 
+        nc.vector.tensor_copy(out=ebar_wide[:], in_=ebar_rows[:])
         warm(14)
+        turn_set(0)
+        turn_set(1)
+        gather_set(0, "scalar")
+        gather_set(1, "vector")
+        quantise_set(0)
+        quantise_set(1)
+        warm(3)
+        turn_set(2)
+        turn_set(3)
+        gather_set(2, "scalar")
+        gather_set(3, "vector")
+        quantise_set(2)
+        quantise_set(3)
         turn_ebar()
-        sort_c(0, "vector")
-        sort_a(0, "vector")
-        turn_cases(0, ["scalar", "scalar"])
-        warm(6)
-        sort_c(1, "vector")
-        quantise_cases(0)
-        turn_cases(1, ["scalar", "vector"])
-        quantise_cases(1)
         spread_contrast(["scalar", "scalar"])
         strain_matmuls(0, 0, (0, 1, 2))
-        turn_cases(2, ["scalar", "scalar"])
-        quantise_cases(2)
+        sort_words(c_sorted[:], c_sb[TILES - 1][:])
+        turn_set(4)
+        turn_set(5)
+        gather_set(4, "scalar")
+        gather_set(5, "vector")
+        quantise_set(4)
+        quantise_set(5)
         strain_matmuls(1, 0, (0, 1, 2))
+        sort_words(a_sorted[:], a_sb[:])
+        turn_set(6)
+        turn_set(7)
+        gather_set(6, "scalar")
+        gather_set(7, "vector")
+        quantise_set(6)
+        quantise_set(7)
         strain_matmuls(2, 0, (0, 1, 2))
         interleave_b(0, ["vector", "scalar"])
+        turn_set(8)
+        turn_set(9)
+        gather_set(8, "scalar")
         quantise_b(0)
-        turn_cases(3, ["scalar", "scalar"])
-        quantise_cases(3)
+        gather_set(9, "vector")
+        quantise_set(8)
+        quantise_set(9)
+        strain_matmuls(3, 0, (0, 1, 2))
+        strain_matmuls(0, 1, (0, 1, 2))
+        strain_matmuls(1, 1, (0, 1, 2))
+        interleave_b(1, ["vector", "scalar"])
         strain_matmuls(0, 0, (3,))
         strain_matmuls(1, 0, (3,))
         strain_matmuls(2, 0, (3,))
-        polarise(0, 0)
-        interleave_b(1, ["vector", "scalar"])
-        strain_matmuls(3, 0)
+        strain_matmuls(3, 0, (3,))
         quantise_b(1)
+        polarise(0, 0)
         polarise(1, 0)
         polarise(2, 0)
         polarise(3, 0)
@@ -459,9 +507,9 @@ def tile_polarisation_green_step_k6_kernel(
             turned = [0, 1] if g == 2 else []
             if more:
                 interleave_b(g + 1, ["scalar"])
-            for m in range(2):
+            for m in range(2 if g == 1 else 0, AHEAD):
                 strain_matmuls(m, g, (0, 1, 2))
-            for m in range(2):
+            for m in range(AHEAD):
                 strain_matmuls(m, g, (3,))
                 polarise(m, g)
             for done in turned:
@@ -470,8 +518,8 @@ def tile_polarisation_green_step_k6_kernel(
             if more:
                 quantise_b(g + 1)
             else:
-                nc.vector.tensor_scalar(out=v_neg[:], in0=v_wide[:], scalar1=-1.0, scalar2=None, op0=ALU.mult)
-            for m in range(2, TILES):
+                negate_v(0)
+            for m in range(AHEAD, TILES):
                 strain_matmuls(m, g)
                 polarise(m, g)
             for done in turned:
@@ -481,7 +529,8 @@ def tile_polarisation_green_step_k6_kernel(
         green_matmuls(0, 0, [0, 1])
         for done in (2, 3):
             for h in range(2):
-                turn_tau(done, h, "scalar" if h == 0 else "vector")
+                turn_tau(done, h, "vector" if (done, h) == (3, 0) else "scalar")
+        for done in (2, 3):
             for h in range(2):
                 quantise_tau(done, h)
         for m in range(1, TILES):
@@ -494,30 +543,35 @@ def tile_polarisation_green_step_k6_kernel(
         every = list(range(PT_CHUNKS))
         last = N_CHUNKS - 1
         for n in range(1, N_CHUNKS):
-            green_matmuls(0, n, every)
-            weigh(0, n)
+            negate_v(n)
+            for m in range(2):
+                green_matmuls(m, n, every)
+                weigh(m, n)
+            round_y(0, n)
             for pair in ([0, 1], [2, 3]):
                 turn_y(n - 1, pair)
                 gather_y(n - 1, pair, "scalar")
-            round_y(0, n)
-            green_matmuls(1, n, every)
-            quantise_y(n - 1, [0, 1])
-            weigh(1, n)
             round_y(1, n)
-            quantise_y(n - 1, [2, 3])
-            store_y_words(n - 1, [0, 1, 2, 3])
-            store_y_scales(n - 1, [nc.sync])
-            for m in range(2, TILES if n < last else TILES - 1):
-                green_matmuls(m, n, every)
-                weigh(m, n)
-                round_y(m, n)
+            quantise_y(n - 1, [0, 1])
+            green_matmuls(2, n, every)
+            weigh(2, n)
+            round_y(2, n)
+            if n < last:
+                finish_chunk(n - 1)
+                store_y_scales(n - 1, 1, [nc.sync])
+                green_matmuls(3, n, every)
+                weigh(3, n)
+                round_y(3, n)
 
-        y = sb("y3", [P, W], F32, bufs=2)
-        rounded = sb("y_half3", [P, W], BF16, bufs=2)
-        y_half[3, last] = rounded
+        y_sb[3, last] = sb("y3", [P, W], F32, bufs=2)
+        y_half[3, last] = sb("y_half3", [P, W], BF16, bufs=2)
         for k in range(2):
-            last_half(3, last, k, y, rounded)
-        nc.sync.dma_start(out=case_rows(out_0, 3)[:, W * last :], in_=y[:])
+            green_half(3, last, k)
+            weigh_half_rounded(3, last, k)
+        finish_chunk(last - 1)
+        for k in range(2):
+            weigh_half(3, last, k)
+        nc.sync.dma_start(out=case_rows(out_0, 3)[:, W * last :], in_=y_sb[3, last][:])
         turn_y(last, [0, 1])
         gather_y(last, [0, 1], "scalar")
         turn_y(last, [2])
@@ -529,4 +583,4 @@ def tile_polarisation_green_step_k6_kernel(
         quantise_y(last, [2])
         quantise_y(last, [3])
         store_y_words(last, [2, 3])
-        store_y_scales(last, [nc.scalar, nc.sync])
+        store_y_scales(last - 1, 2, [nc.scalar, nc.sync])

@@ -19,7 +19,7 @@ P = 128
 W = 512
 TILES = 4
 BANKS = 8
-AHEAD = 3
+AHEAD = {1: 4, 2: 2, 3: 2}
 C_PASSES = Q // W
 PT_CHUNKS = PTS // W
 N_CHUNKS = N // W
@@ -99,12 +99,17 @@ def tile_polarisation_green_step_k6_kernel(
         con_wide = [sb("con_wide%d" % u, [P, PTS // 2], BF16) for u in range(2)]
         a_sb = sb("a_sb", [P, TILES * R], BF16)
         c_sb = [sb("c%d" % m, [P, Q], BF16) for m in range(TILES)]
+        c_first = sb("c_first", [P, 2 * W], BF16)
         b_sb = [sb("b%d" % g, [P, 4, W], BF16) for g in range(PT_CHUNKS)]
         d_sb = [sb("d%d" % g, [P, C_PASSES, 2 * W], U8) for g in range(PT_CHUNKS)]
         g_sb = [sb("g%d" % n, [P, PT_CHUNKS, W], U32) for n in range(N_CHUNKS)]
 
         def load_c(m):
-            nc.sync.dma_start(out=c_sb[m][:], in_=case_rows(c, m))
+            if m == 0:
+                nc.sync.dma_start(out=c_first[:], in_=case_rows(c, m)[:, : 2 * W])
+                nc.sync.dma_start(out=c_sb[m][:, 2 * W :], in_=case_rows(c, m)[:, 2 * W :])
+            else:
+                nc.sync.dma_start(out=c_sb[m][:], in_=case_rows(c, m))
 
         def load_a():
             nc.sync.dma_start(
@@ -199,7 +204,8 @@ def tile_polarisation_green_step_k6_kernel(
                 return a_sorted[:, 2 * P * m + P * u : 2 * P * m + P * (u + 1)]
             if m == TILES - 1:
                 return c_sorted[:, 2 * P * j + P * u : 2 * P * j + P * (u + 1)]
-            return c_sb[m][:].bitcast(F32)[:, 2 * P * j + u : 2 * P * (j + 1) : 2]
+            source = c_first if m == 0 and j < 2 else c_sb[m]
+            return source[:].bitcast(F32)[:, 2 * P * j + u : 2 * P * (j + 1) : 2]
 
         def turn_set(k):
             ac_bank[k] = new_bank(("cases", k))
@@ -504,27 +510,28 @@ def tile_polarisation_green_step_k6_kernel(
 
         for g in range(1, PT_CHUNKS):
             more = g + 1 < PT_CHUNKS
-            turned = [0, 1] if g == 2 else []
             if more:
                 interleave_b(g + 1, ["scalar"])
-            for m in range(2 if g == 1 else 0, AHEAD):
+            ahead = AHEAD[g]
+            for m in range(2 if g == 1 else 0, ahead):
                 strain_matmuls(m, g, (0, 1, 2))
-            for m in range(AHEAD):
-                strain_matmuls(m, g, (3,))
-                polarise(m, g)
-            for done in turned:
-                for h in range(2):
-                    turn_tau(done, h, "scalar")
             if more:
                 quantise_b(g + 1)
             else:
                 negate_v(0)
-            for m in range(AHEAD, TILES):
+                for done in (0, 1):
+                    for h in range(2):
+                        quantise_tau(done, h)
+            for m in range(ahead):
+                strain_matmuls(m, g, (3,))
+                polarise(m, g)
+            for m in range(ahead, TILES):
                 strain_matmuls(m, g)
                 polarise(m, g)
-            for done in turned:
-                for h in range(2):
-                    quantise_tau(done, h)
+            if g == 2:
+                for done in (0, 1):
+                    for h in range(2):
+                        turn_tau(done, h, "scalar")
 
         green_matmuls(0, 0, [0, 1])
         for done in (2, 3):
@@ -575,9 +582,9 @@ def tile_polarisation_green_step_k6_kernel(
         turn_y(last, [0, 1])
         gather_y(last, [0, 1], "scalar")
         turn_y(last, [2])
-        gather_y(last, [2], "scalar")
+        gather_y(last, [2], "vector")
         turn_y(last, [3])
-        gather_y(last, [3], "vector")
+        gather_y(last, [3], "scalar")
         quantise_y(last, [0, 1])
         store_y_words(last, [0, 1])
         quantise_y(last, [2])

from contextlib import ExitStack

import concourse.mybir as mybir
from concourse.masks import make_identity

S, R, Q, PTS, N = 512, 512, 1536, 2048, 1536
FLOPS = 2 * S * (R + Q) * PTS + 2 * S * PTS * N

F32 = mybir.dt.float32
BF16 = mybir.dt.bfloat16
I32 = mybir.dt.int32
U32 = mybir.dt.uint32
U8 = mybir.dt.uint8
FP8X4 = mybir.dt.float8_e4m3fn_x4
FP4X4 = mybir.dt.float4_e2m1fn_x4
ALU = mybir.AluOpType

P = 128
W = 512
TILES = 4
BANKS = 8
AHEAD = {1: 4, 2: 2, 3: 2}
C_PASSES = Q // W
PT_CHUNKS = PTS // W
N_CHUNKS = N // W


def tile_polarisation_green_step_k6_kernel(
    tc, a, b, c, d_words, d_scales, ebar, contrast, gam_words, gam_scales, v, out_0, out_1, out_2
):
    nc = tc.nc
    with ExitStack() as ctx:
        keep = ctx.enter_context(tc.tile_pool(name="keep", bufs=1))
        psum = ctx.enter_context(tc.psum_pool(name="psum", bufs=1))
        ctx.enter_context(tc.manual_schedule())

        free_banks = list(range(BANKS))
        bank_index = {}

        def new_bank(key):
            index = free_banks[0]
            free_banks.remove(index)
            bank_index[key] = index
            return psum.tile([P, W], F32, name="bank%d" % index)

        def release(key):
            free_banks.append(bank_index[key])

        def sb(name, shape, dtype, bufs=1):
            return keep.tile(shape, dtype, name=name, bufs=bufs, align_bytes=256)

        def copy(engine, out, in_):
            if engine == "vector":
                nc.vector.tensor_copy(out=out, in_=in_)
            else:
                nc.scalar.copy(out=out, in_=in_)

        def case_rows(ap, m):
            return ap[P * m : P * (m + 1), :]

        ident = sb("ident", [P, P], F32)
        make_identity(nc, ident[:])

        warm_in = sb("warm_in", [P, W], BF16)
        warm_codes = sb("warm_codes", [P, P], U32)
        warm_scales = sb("warm_scales", [P, P], U8)
        ebar_rows = sb("ebar_rows", [P, P], BF16)
        ebar_wide = sb("ebar_wide", [P, P], F32)
        nc.vector.memset(warm_in[:], 1.0)
        nc.vector.memset(ebar_rows[:], 0.0)
        d_plane0 = sb("d_plane0", [P, C_PASSES, W], U8)
        d_plane1 = sb("d_plane1", [P, C_PASSES, W], U8)
        d_plane2 = sb("d_plane2", [P, C_PASSES, 2 * W], U8)
        g_plane = sb("g_plane", [P, N], U8)
        nc.vector.memset(d_plane0[:].rearrange("p j n -> p (j n)").bitcast(I32), 0)
        nc.vector.quantize_mx(out=warm_codes[:].bitcast(FP8X4), scales=warm_scales[:], in_=warm_in[:])
        warm_bank = new_bank("warm")

        def warm(count):
            for unused in range(count):
                nc.tensor.matmul_mx(
                    out=warm_bank[:, :P],
                    lhsT=warm_codes[:].bitcast(FP8X4),
                    lhsT_scale=warm_scales[:],
                    rhs=warm_codes[:].bitcast(FP8X4),
                    rhs_scale=warm_scales[:],
                    start=True,
                    stop=True,
                )

        nc.vector.memset(d_plane1[:].rearrange("p j n -> p (j n)").bitcast(I32), 0)
        nc.vector.memset(d_plane2[:].rearrange("p j n -> p (j n)").bitcast(I32), 0)
        nc.vector.memset(g_plane[:].bitcast(I32), 0)

        con_rows = sb("con_rows", [P, PTS // P], BF16)
        ebar_sb = sb("ebar_sb", [P, TILES], F32)
        v_wide = [sb("v_wide%d" % n, [P, W], BF16) for n in range(N_CHUNKS)]
        v_neg = [sb("v_neg%d" % n, [P, W], BF16) for n in range(N_CHUNKS)]
        con_wide = [sb("con_wide%d" % u, [P, PTS // 2], BF16) for u in range(2)]
        a_sb = sb("a_sb", [P, TILES * R], BF16)
        c_sb = [sb("c%d" % m, [P, Q], BF16) for m in range(TILES)]
        c_first = sb("c_first", [P, 2 * W], BF16)
        b_sb = [sb("b%d" % g, [P, 4, W], BF16) for g in range(PT_CHUNKS)]
        d_sb = [sb("d%d" % g, [P, C_PASSES, 2 * W], U8) for g in range(PT_CHUNKS)]
        g_sb = [sb("g%d" % n, [P, PT_CHUNKS, W], U32) for n in range(N_CHUNKS)]

        def load_c(m):
            if m == 0:
                nc.sync.dma_start(out=c_first[:], in_=case_rows(c, m)[:, : 2 * W])
                nc.sync.dma_start(out=c_sb[m][:, 2 * W :], in_=case_rows(c, m)[:, 2 * W :])
            else:
                nc.sync.dma_start(out=c_sb[m][:], in_=case_rows(c, m))

        def load_a():
            nc.sync.dma_start(
                out=a_sb[:].rearrange("i (m k) -> i m k", m=TILES), in_=a.rearrange("(m i) k -> i m k", m=TILES)
            )

        def load_b(g):
            nc.sync.dma_start(out=b_sb[g][:], in_=b[:, W * g : W * (g + 1)].rearrange("(p t) n -> p t n", t=4))

        def load_d(g):
            src = d_words.rearrange("j p n -> p j n")[:, :, 2 * W * g : 2 * W * (g + 1)]
            nc.sync.dma_start(out=d_sb[g][:].bitcast(I32), in_=src.bitcast(I32))

        def load_d_scales(queue, plane, first, last):
            for r in range(4):
                src = d_scales[:, r:16:4, first:last].rearrange("j q n -> q j n")
                queue.dma_start(out=plane[r:P:32, :, :].bitcast(I32), in_=src.bitcast(I32))

        def load_gam(n):
            src = gam_words.rearrange("g p n t -> p g (n t)")[:, :, 4 * W * n : 4 * W * (n + 1)]
            nc.sync.dma_start(out=g_sb[n][:].bitcast(I32), in_=src.bitcast(I32))

        nc.scalar.dma_start(out=con_rows[:], in_=contrast.rearrange("(p c) -> p c", p=P))
        nc.scalar.dma_start(out=ebar_rows[:TILES, :], in_=ebar.rearrange("(m i) -> m i", m=TILES))
        load_c(0)
        load_c(1)
        load_d_scales(nc.scalar, d_plane0, 0, W)
        load_d(0)
        load_c(2)
        load_c(3)
        load_a()
        load_b(0)
        load_d_scales(nc.sync, d_plane1, W, 2 * W)
        load_d(1)
        load_b(1)
        load_b(2)
        load_d_scales(nc.sync, d_plane2, 2 * W, PTS)
        load_d(2)
        load_b(3)
        load_d(3)
        for q in range(4):
            nc.sync.dma_start(
                out=g_plane[32 * q : 32 * q + 16, :].bitcast(I32),
                in_=gam_scales[:, 4 * q : 4 * q + 4, :].bitcast(I32),
            )
        for n in range(N_CHUNKS):
            load_gam(n)
            nc.sync.dma_start(out=v_wide[n][:], in_=v[W * n : W * (n + 1)].partition_broadcast(P))

        def turn_ebar():
            nc.tensor.transpose(warm_bank[:, P : 2 * P], ebar_wide[:], ident[:])
            nc.scalar.copy(out=ebar_sb[:], in_=warm_bank[:, P : P + TILES])
            release("warm")

        def spread_contrast(engines):
            words = con_rows[:].bitcast(F32)
            for u in range(2):
                bank = new_bank("contrast")
                for k in range(4):
                    col = 2 * k + u
                    nc.tensor.transpose(
                        bank[:, P * k : P * (k + 1)], words[:, col : col + 1].to_broadcast([P, P]), ident[:]
                    )
                copy(
                    engines[u],
                    con_wide[u][:].bitcast(F32).rearrange("j (r k) -> j r k", k=4),
                    bank[:].rearrange("j (k r) -> j r k", k=4),
                )
                release("contrast")

        sets = []
        for m in range(TILES):
            sets.extend([[(m, 0), (m, 1)], [(m, 2)]])
        sets.extend([[(0, 3), (1, 3)], [(2, 3), (3, 3)]])
        place = {unit: (k, side) for k, units in enumerate(sets) for side, unit in enumerate(units)}
        ac_codes = [sb("ac_codes%d" % k, [P, P * len(units)], U32) for k, units in enumerate(sets)]
        ac_scales = [sb("ac_scales%d" % k, [P, P * len(units)], U8) for k, units in enumerate(sets)]
        ac_bank = {}
        ac_grouped = {}

        c_sorted = sb("c_sorted", [P, Q // 2], F32)
        a_sorted = sb("a_sorted", [P, TILES * R // 2], F32)

        def sort_words(out, in_):
            nc.vector.tensor_copy(
                out=out.rearrange("s (j u r i) -> s j r u i", u=2, r=32, i=4),
                in_=in_.bitcast(F32).rearrange("s (j r i u) -> s j r u i", u=2, r=32, i=4),
            )

        def unit_words(m, j, u):
            if j == C_PASSES:
                return a_sorted[:, 2 * P * m + P * u : 2 * P * m + P * (u + 1)]
            if m == TILES - 1:
                return c_sorted[:, 2 * P * j + P * u : 2 * P * j + P * (u + 1)]
            source = c_first if m == 0 and j < 2 else c_sb[m]
            return source[:].bitcast(F32)[:, 2 * P * j + u : 2 * P * (j + 1) : 2]

        def turn_set(k):
            ac_bank[k] = new_bank(("cases", k))
            for side, (m, j) in enumerate(sets[k]):
                for u in range(2):
                    slot = 2 * side + u
                    nc.tensor.transpose(ac_bank[k][:, P * slot : P * (slot + 1)], unit_words(m, j, u), ident[:])

        def gather_set(k, engine):
            count = len(sets[k])
            grouped = sb("ac_grouped%d" % count, [P, W * count], BF16, bufs=3)
            ac_grouped[k] = grouped
            copy(
                engine,
                grouped[:].bitcast(F32).rearrange("p (j i u) -> p j i u", i=P, u=2),
                ac_bank[k][:, : 2 * P * count].rearrange("p (j u i) -> p j i u", i=P, u=2),
            )
            release(("cases", k))

        def quantise(codes, scales, grouped):
            nc.vector.quantize_mx(out=codes.bitcast(FP8X4), scales=scales, in_=grouped)

        def quantise_set(k):
            quantise(ac_codes[k][:], ac_scales[k][:], ac_grouped[k][:])

        b_codes = [sb("b_codes%d" % g, [P, W], U32) for g in range(PT_CHUNKS)]
        b_scales = [sb("b_scales%d" % g, [P, W], U8) for g in range(PT_CHUNKS)]
        b_grouped = {}

        def interleave_b(g, engines):
            grouped = sb("b_grouped", [P, 4 * W], BF16, bufs=2)
            b_grouped[g] = grouped
            share = W // len(engines)
            for s, engine in enumerate(engines):
                copy(
                    engine,
                    grouped[:, 4 * share * s : 4 * share * (s + 1)].rearrange("p (c i t) -> p c t i", i=4, t=4),
                    b_sb[g][:, :, share * s : share * (s + 1)].rearrange("p t (c i) -> p c t i", i=4),
                )

        def quantise_b(g):
            quantise(b_codes[g][:], b_scales[g][:], b_grouped[g][:])

        strain_bank = {}

        def strain_matmuls(m, g, passes=(0, 1, 2, 3)):
            if passes[0] == 0:
                strain_bank[m, g] = new_bank(("strain", m, g))
            bank = strain_bank[m, g]
            for j in passes:
                k, side = place[m, j]
                cols = slice(P * side, P * (side + 1))
                if j == C_PASSES:
                    rhs, rhs_scale = b_codes[g][:].bitcast(FP8X4), b_scales[g][:]
                elif g == 0:
                    rhs, rhs_scale = d_sb[g][:, j, :].bitcast(FP4X4), d_plane0[:, j, :]
                elif g == 1:
                    rhs, rhs_scale = d_sb[g][:, j, :].bitcast(FP4X4), d_plane1[:, j, :]
                else:
                    rhs, rhs_scale = d_sb[g][:, j, :].bitcast(FP4X4), d_plane2[:, j, W * (g - 2) : W * (g - 1)]
                nc.tensor.matmul_mx(
                    out=bank[:],
                    lhsT=ac_codes[k][:, cols].bitcast(FP8X4),
                    lhsT_scale=ac_scales[k][:, cols],
                    rhs=rhs,
                    rhs_scale=rhs_scale,
                    start=(j == 0),
                    stop=(j == C_PASSES),
                )

        def sorted_pairs(ap, u):
            return ap.rearrange("s (p u e) -> s u p e", u=2, e=2)[:, u]

        tau_sb = {}

        def polarise(m, g):
            tau = sb("tau%d" % m, [P, W], BF16, bufs=3)
            tau_sb[m, g] = tau
            for u in range(2):
                half = slice(2 * P * g, 2 * P * (g + 1))
                nc.vector.scalar_tensor_tensor(
                    out=tau[:, 2 * P * u : 2 * P * (u + 1)].rearrange("s (p e) -> s p e", e=2),
                    in0=sorted_pairs(strain_bank[m, g][:], u),
                    scalar=ebar_sb[:, m : m + 1],
                    in1=con_wide[u][:, half].rearrange("s (p e) -> s p e", e=2),
                    op0=ALU.add,
                    op1=ALU.mult,
                )
            release(("strain", m, g))

        def turn_tile(bank, e, source):
            words = source[:].bitcast(F32)
            for u in range(2):
                slot = 2 * e + u
                nc.tensor.transpose(bank[:, P * slot : P * (slot + 1)], words[:, P * u : P * (u + 1)], ident[:])

        tau_codes = [sb("tau_codes%d" % g, [P, W], U32) for g in range(PT_CHUNKS)]
        tau_scales = [sb("tau_scales%d" % g, [P, W], U8) for g in range(PT_CHUNKS)]
        tau_grouped = {}

        def turn_tau(g, h, engine):
            bank = new_bank("tau")
            for e in range(2):
                turn_tile(bank, e, tau_sb[2 * h + e, g])
            grouped = sb("tau_grouped%d" % h, [P, 2 * W], BF16, bufs=2)
            tau_grouped[g, h] = grouped
            copy(
                engine,
                grouped[:].bitcast(F32).rearrange("p (e i u) -> p e i u", e=2, u=2),
                bank[:].rearrange("p (e u i) -> p e i u", e=2, u=2),
            )
            release("tau")

        def quantise_tau(g, h):
            cols = slice(2 * P * h, 2 * P * (h + 1))
            quantise(tau_codes[g][:, cols], tau_scales[g][:, cols], tau_grouped[g, h][:])

        green_bank = {}

        def green_matmuls(m, n, passes):
            if passes[0] == 0:
                green_bank[m, n] = new_bank(("green", m, n))
            cols = slice(P * m, P * (m + 1))
            for g in passes:
                nc.tensor.matmul_mx(
                    out=green_bank[m, n][:],
                    lhsT=tau_codes[g][:, cols].bitcast(FP8X4),
                    lhsT_scale=tau_scales[g][:, cols],
                    rhs=g_sb[n][:, g, :].bitcast(FP8X4),
                    rhs_scale=g_plane[4 * g :, W * n : W * (n + 1)],
                    start=(g == 0),
                    stop=(g == PT_CHUNKS - 1),
                )

        def negate_v(n):
            nc.vector.tensor_scalar(out=v_neg[n][:], in0=v_wide[n][:], scalar1=-1.0, scalar2=None, op0=ALU.mult)

        y_sb = {}
        y_half = {}

        def weigh(m, n):
            y = sb("y%d" % m, [P, W], F32, bufs=2)
            y_sb[m, n] = y
            nc.vector.scalar_tensor_tensor(
                out=y[:],
                in0=green_bank[m, n][:],
                scalar=ebar_sb[:, m : m + 1],
                in1=v_neg[n][:],
                op0=ALU.subtract,
                op1=ALU.mult,
            )
            release(("green", m, n))
            nc.sync.dma_start(out=case_rows(out_0, m)[:, W * n : W * (n + 1)], in_=y[:])

        def round_y(m, n):
            rounded = sb("y_half%d" % m, [P, W], BF16, bufs=2)
            y_half[m, n] = rounded
            nc.scalar.copy(
                out=rounded[:].rearrange("s (u r i e) -> s r u i e", u=2, i=4, e=2),
                in_=y_sb[m, n][:].rearrange("s (r i u e) -> s r u i e", u=2, i=4, e=2),
            )

        y_codes = [sb("y_codes%d" % n, [P, W], U32) for n in range(N_CHUNKS)]
        y_scales = sb("y_scales", [P, N], U8)
        y_turned = {}
        y_grouped = {}

        def turn_y(n, tiles):
            bank = new_bank(("y", n, tiles[0]))
            y_turned[n, tiles[0]] = bank
            for e, m in enumerate(tiles):
                turn_tile(bank, e, y_half[m, n])

        def gather_y(n, tiles, engine):
            width = 2 * P * len(tiles)
            grouped = sb("y_grouped%d" % len(tiles), [P, 2 * width], BF16, bufs=2)
            y_grouped[n, tiles[0]] = grouped
            copy(
                engine,
                grouped[:].bitcast(F32).rearrange("p (e i u) -> p e i u", i=P, u=2),
                y_turned[n, tiles[0]][:, :width].rearrange("p (e u i) -> p e i u", i=P, u=2),
            )
            release(("y", n, tiles[0]))

        def quantise_y(n, tiles):
            cols = slice(P * tiles[0], P * (tiles[-1] + 1))
            plane = y_scales[:, W * n : W * (n + 1)]
            quantise(y_codes[n][:, cols], plane[:, cols], y_grouped[n, tiles[0]][:])

        def store_y_words(n, tiles):
            cols = slice(P * tiles[0], P * (tiles[-1] + 1))
            nc.sync.dma_start(
                out=out_1[n].rearrange("p m t -> p (m t)").bitcast(I32)[:, cols], in_=y_codes[n][:, cols].bitcast(I32)
            )

        def store_y_scales(first, count, queues):
            for r in range(4):
                rows = y_scales[r:P:32, W * first : W * (first + count)]
                queues[r % len(queues)].dma_start(
                    out=out_2[first : first + count, r:16:4, :].rearrange("n q m -> q n m").bitcast(I32),
                    in_=rows.rearrange("q (n m) -> q n m", m=W).bitcast(I32),
                )

        def finish_chunk(n):
            quantise_y(n, [2, 3])
            store_y_words(n, [0, 1, 2, 3])

        half_bank = {}

        def green_half(m, n, k):
            bank = new_bank(("half", k))
            half_bank[k] = bank
            cols = slice(P * m, P * (m + 1))
            for g in range(PT_CHUNKS):
                nc.tensor.matmul_mx(
                    out=bank[:, : 2 * P],
                    lhsT=tau_codes[g][:, cols].bitcast(FP8X4),
                    lhsT_scale=tau_scales[g][:, cols],
                    rhs=g_sb[n][:, g, 2 * P * k : 2 * P * (k + 1)].bitcast(FP8X4),
                    rhs_scale=g_plane[4 * g :, W * n + 2 * P * k : W * n + 2 * P * (k + 1)],
                    start=(g == 0),
                    stop=(g == PT_CHUNKS - 1),
                )

        def weigh_half_rounded(m, n, k):
            for u in range(2):
                nc.vector.scalar_tensor_tensor(
                    out=y_half[m, n][:, 2 * P * u + P * k : 2 * P * u + P * (k + 1)].rearrange("s (p e) -> s p e", e=2),
                    in0=sorted_pairs(half_bank[k][:, : 2 * P], u),
                    scalar=ebar_sb[:, m : m + 1],
                    in1=sorted_pairs(v_neg[n][:, 2 * P * k : 2 * P * (k + 1)], u),
                    op0=ALU.subtract,
                    op1=ALU.mult,
                )

        def weigh_half(m, n, k):
            part = slice(2 * P * k, 2 * P * (k + 1))
            nc.vector.scalar_tensor_tensor(
                out=y_sb[m, n][:, part],
                in0=half_bank[k][:, : 2 * P],
                scalar=ebar_sb[:, m : m + 1],
                in1=v_neg[n][:, part],
                op0=ALU.subtract,
                op1=ALU.mult,
            )

        nc.vector.tensor_copy(out=ebar_wide[:], in_=ebar_rows[:])
        warm(14)
        turn_set(0)
        turn_set(1)
        gather_set(0, "scalar")
        gather_set(1, "vector")
        quantise_set(0)
        quantise_set(1)
        warm(3)
        turn_set(2)
        turn_set(3)
        gather_set(2, "scalar")
        gather_set(3, "vector")
        quantise_set(2)
        quantise_set(3)
        turn_ebar()
        spread_contrast(["scalar", "scalar"])
        strain_matmuls(0, 0, (0, 1, 2))
        sort_words(c_sorted[:], c_sb[TILES - 1][:])
        turn_set(4)
        turn_set(5)
        gather_set(4, "scalar")
        gather_set(5, "vector")
        quantise_set(4)
        quantise_set(5)
        strain_matmuls(1, 0, (0, 1, 2))
        sort_words(a_sorted[:], a_sb[:])
        turn_set(6)
        turn_set(7)
        gather_set(6, "scalar")
        gather_set(7, "vector")
        quantise_set(6)
        quantise_set(7)
        strain_matmuls(2, 0, (0, 1, 2))
        interleave_b(0, ["vector", "scalar"])
        turn_set(8)
        turn_set(9)
        gather_set(8, "scalar")
        quantise_b(0)
        gather_set(9, "vector")
        quantise_set(8)
        quantise_set(9)
        strain_matmuls(3, 0, (0, 1, 2))
        strain_matmuls(0, 1, (0, 1, 2))
        strain_matmuls(1, 1, (0, 1, 2))
        interleave_b(1, ["vector", "scalar"])
        strain_matmuls(0, 0, (3,))
        strain_matmuls(1, 0, (3,))
        strain_matmuls(2, 0, (3,))
        strain_matmuls(3, 0, (3,))
        quantise_b(1)
        polarise(0, 0)
        polarise(1, 0)
        polarise(2, 0)
        polarise(3, 0)

        for g in range(1, PT_CHUNKS):
            more = g + 1 < PT_CHUNKS
            if more:
                interleave_b(g + 1, ["scalar"])
            ahead = AHEAD[g]
            for m in range(2 if g == 1 else 0, ahead):
                strain_matmuls(m, g, (0, 1, 2))
            if more:
                quantise_b(g + 1)
            else:
                negate_v(0)
                for done in (0, 1):
                    for h in range(2):
                        quantise_tau(done, h)
            for m in range(ahead):
                strain_matmuls(m, g, (3,))
                polarise(m, g)
            for m in range(ahead, TILES):
                strain_matmuls(m, g)
                polarise(m, g)
            if g == 2:
                for done in (0, 1):
                    for h in range(2):
                        turn_tau(done, h, "scalar")

        green_matmuls(0, 0, [0, 1])
        for done in (2, 3):
            for h in range(2):
                turn_tau(done, h, "vector" if (done, h) == (3, 0) else "scalar")
        for done in (2, 3):
            for h in range(2):
                quantise_tau(done, h)
        for m in range(1, TILES):
            green_matmuls(m, 0, [0, 1])
        for m in range(TILES):
            green_matmuls(m, 0, [2, 3])
            weigh(m, 0)
            round_y(m, 0)

        every = list(range(PT_CHUNKS))
        last = N_CHUNKS - 1
        for n in range(1, N_CHUNKS):
            negate_v(n)
            for m in range(2):
                green_matmuls(m, n, every)
                weigh(m, n)
            round_y(0, n)
            for pair in ([0, 1], [2, 3]):
                turn_y(n - 1, pair)
                gather_y(n - 1, pair, "scalar")
            round_y(1, n)
            quantise_y(n - 1, [0, 1])
            green_matmuls(2, n, every)
            weigh(2, n)
            round_y(2, n)
            if n < last:
                finish_chunk(n - 1)
                store_y_scales(n - 1, 1, [nc.sync])
                green_matmuls(3, n, every)
                weigh(3, n)
                round_y(3, n)

        y_sb[3, last] = sb("y3", [P, W], F32, bufs=2)
        y_half[3, last] = sb("y_half3", [P, W], BF16, bufs=2)
        for k in range(2):
            green_half(3, last, k)
            weigh_half_rounded(3, last, k)
        finish_chunk(last - 1)
        for k in range(2):
            weigh_half(3, last, k)
        nc.sync.dma_start(out=case_rows(out_0, 3)[:, W * last :], in_=y_sb[3, last][:])
        turn_y(last, [0, 1])
        gather_y(last, [0, 1], "scalar")
        turn_y(last, [2])
        gather_y(last, [2], "vector")
        turn_y(last, [3])
        gather_y(last, [3], "scalar")
        quantise_y(last, [0, 1])
        store_y_words(last, [0, 1])
        quantise_y(last, [2])
        quantise_y(last, [3])
        store_y_words(last, [2, 3])
        store_y_scales(last - 1, 2, [nc.scalar, nc.sync])
